import numpy as np
import ml_dtypes


def mxq(x, axis, fmt="e4m3"):
    dtype, down = {"e4m3": (ml_dtypes.float8_e4m3fn, 7), "e5m2": (ml_dtypes.float8_e5m2, 14)}[fmt]
    v = np.moveaxis(np.asarray(x, np.float32).astype(ml_dtypes.bfloat16).astype(np.float64), axis, -1)
    blocks = v.reshape(v.shape[:-1] + (-1, 32))
    amax = np.abs(blocks).max(-1, keepdims=True)
    byte = np.maximum(np.where(amax > 0, np.frexp(amax)[1] - 1 + 127, 0) - down, 1)
    scale = np.exp2(byte - 127.0)
    codes = (blocks / scale).astype(np.float32).astype(dtype).astype(np.float64)
    return np.moveaxis((codes * scale).reshape(v.shape), -1, axis)


WIDE = False


def mx_kscale(k):
    if not WIDE:
        return np.ones(k)
    levels = np.array([10, -10, 5, -5, 0])
    if k % 512:
        return np.exp2(np.random.permutation(np.resize(levels, k // 32))).repeat(32)
    a = np.empty((k // 512, 16))
    for p in range(k // 512):
        a[p, :8] = np.random.permutation(np.resize(levels, 8))
        for g in range(8):
            far = levels[np.abs(levels - a[p, g]) >= 10]
            a[p, g + 8] = far[np.random.randint(len(far))]
    return np.exp2(a.ravel()).repeat(32)


def f64(x):
    return np.asarray(x).astype(np.float64)


def striped(idx):
    return np.tile(idx.reshape(-1, 16).T, (8, 1)).astype(np.uint16)


def unstriped(offs):
    return offs[:16].T.reshape(-1).astype(np.int64)


E2M1 = np.array([0.0, 0.5, 1.0, 1.5, 2.0, 3.0, 4.0, 6.0, -0.0, -0.5, -1.0, -1.5, -2.0, -3.0, -4.0, -6.0])


def pack_weight(w, fmt):
    k, n = w.shape
    w = f64(np.asarray(w, np.float32).astype(ml_dtypes.bfloat16)).reshape(k // 32, 32, n)
    amax = np.abs(w).max(1)
    if fmt == "e4m3":
        byte = np.frexp(amax)[1] - 1 + 127 - 7
    else:
        mant, ex = np.frexp(amax / 6.0)
        byte = np.where(mant > 0.5, ex, ex - 1) + 127
    byte = np.clip(np.where(amax > 0, byte, 1), 1, 254)
    scaled = (w * np.exp2(127.0 - byte)[:, None, :]).reshape(k, n).astype(np.float32)
    by_word = np.ascontiguousarray(scaled.reshape(k // 512, 128, 4, n).transpose(0, 1, 3, 2))
    if fmt == "e4m3":
        words = by_word.astype(ml_dtypes.float8_e4m3fn).view(np.uint8)
    else:
        c = by_word.astype(ml_dtypes.float4_e2m1fn).view(np.uint8) & 0xF
        words = (c[..., 0::2] | (c[..., 1::2] << 4)).reshape(k // 512, 128, 2 * n)
    return np.ascontiguousarray(words), np.ascontiguousarray(byte.astype(np.uint8).reshape(k // 512, 16, n))


def unpack_weight(words, scales, fmt):
    g, _, n = scales.shape
    words = np.ascontiguousarray(words).reshape(g, 128, n, -1)
    if fmt == "e4m3":
        vals = words.view(ml_dtypes.float8_e4m3fn).astype(np.float64)
    else:
        nib = np.empty((g, 128, n, 4), np.uint8)
        nib[..., 0::2] = words & 0xF
        nib[..., 1::2] = words >> 4
        vals = E2M1[nib]
    vals = vals * np.repeat(np.exp2(scales.astype(np.float64) - 127.0), 8, axis=1)[..., None]
    return vals.transpose(0, 1, 3, 2).reshape(g * 512, n)


def gelu(v):
    return 0.5 * v * (1.0 + np.tanh(np.sqrt(2.0 / np.pi) * (v + 0.044715 * v**3)))


K, H, N, T, S, P = 1536, 1024, 640, 2048, 1024, 512

def setup_inputs():
    n = np.random.standard_normal
    s = mx_kscale(K)[:, None]
    u = mx_kscale(H)[:, None]
    tab_words, tab_scales = pack_weight(n((K, T)) * s, "e4m3")
    w3_words, w3_scales = pack_weight(1.3 * n((H, N)) / np.sqrt(K * H / K) / u, "e2m1")
    signs = np.random.choice([-1.0, 1.0], H)
    return {
        "tab_words": tab_words, "tab_scales": tab_scales,
        "offs": striped(np.random.permutation(T)[:S]),
        "pos1": striped(np.random.permutation(S)[:P]),
        "pos2": striped(np.random.permutation(S)[:P]),
        "w1": (0.85 * n((K, H)) / np.sqrt(K) / s).astype(np.float32),
        "quiet": (0.85 * n((H, S))).astype(np.float32),
        "thr": n(H).astype(np.float32),
        "sharp": np.random.uniform(1, 3, H).astype(np.float32),
        "share": np.random.uniform(0.1, 0.5, H).astype(np.float32),
        "side": (signs * np.random.uniform(1.5, 4.0, H) * u[:, 0]).astype(np.float32),
        "w3_words": w3_words, "w3_scales": w3_scales,
        "w4": (0.8 * n((H, N)) / np.sqrt(H) / u).astype(np.float32),
        "duty": n((N, P)).astype(np.float32),
    }

def reference(tab_words, tab_scales, offs, pos1, pos2, w1, quiet, thr, sharp, share, side,
              w3_words, w3_scales, w4, duty):
    v = unpack_weight(tab_words, tab_scales, "e4m3")[:, unstriped(offs)]
    h = np.maximum(mxq(f64(w1), 0, "e4m3").T @ v, f64(quiet))
    a = 1.0 / (1.0 + np.exp(-(h[:, unstriped(pos1)] + f64(thr)[:, None])))
    top = h.max(axis=1)
    c = 1.0 / (1.0 + np.exp(-f64(sharp)[:, None] * (h[:, unstriped(pos2)] - f64(share)[:, None] * top[:, None])))
    d = mxq(f64(side)[:, None] * (a - c), 0, "e4m3")
    alarm = np.tanh(unpack_weight(w3_words, w3_scales, "e2m1").T @ d)
    trend = mxq(f64(w4), 0, "e4m3").T @ d
    return alarm * f64(duty) + trend

@@ -1,0 +1,313 @@
+from contextlib import ExitStack
+
+import concourse.mybir as mybir
+
+K, H, N, T, S, M = 1536, 1024, 640, 2048, 1024, 512
+FLOPS = 2 * K * H * S + 2 * 2 * H * N * M
+
+F32 = mybir.dt.float32
+BF16 = mybir.dt.bfloat16
+I32 = mybir.dt.int32
+U32 = mybir.dt.uint32
+U16 = mybir.dt.uint16
+U8 = mybir.dt.uint8
+FP8X4 = mybir.dt.float8_e4m3fn_x4
+FP4X4 = mybir.dt.float4_e2m1fn_x4
+ALU = mybir.AluOpType
+ACT = mybir.ActivationFunctionType
+AXIS = mybir.AxisListType
+
+P = 128
+PACK = 4
+K_PASS = P * PACK
+BANK = 512
+K_PASSES = K // K_PASS
+R_PASSES = H // K_PASS
+N_TILES = N // P
+HALF = M // 2
+
+
+def tile_list_ammonia_leak_watch_kernel(
+    tc, tab_words, tab_scales, offs, pos1, pos2, w1, quiet, thr, sharp, share, side,
+    w3_words, w3_scales, w4, duty, out,
+):
+    nc = tc.nc
+    with ExitStack() as ctx:
+        lists = ctx.enter_context(tc.tile_pool(name="lists", bufs=1))
+        keep = ctx.enter_context(tc.tile_pool(name="keep", bufs=1))
+        ring = ctx.enter_context(tc.tile_pool(name="ring", bufs=1))
+        psum = ctx.enter_context(tc.psum_pool(name="psum", bufs=8))
+
+        offs_t = lists.tile([P, S // 16], U16, name="offs_t")
+        pos1_t = lists.tile([P, M // 16], U16, name="pos1_t")
+        pos2_t = lists.tile([P, M // 16], U16, name="pos2_t")
+
+        tab_t = [keep.tile([P, T], I32, name="tab%d" % a, align_bytes=64) for a in range(K_PASSES)]
+        tab_sc = keep.tile([P, T], U8, name="tab_sc", align_bytes=64)
+        w3_sc = keep.tile([P, R_PASSES, N], U8, name="w3_sc", align_bytes=64)
+        w3_t = keep.tile([P, R_PASSES, 2 * N], U8, name="w3_t", align_bytes=64)
+        duty_t = keep.tile([P, N_TILES, M], F32, name="duty_t")
+
+        def load_raw(weight, a, cols):
+            raw = ring.tile([P, PACK, cols.stop - cols.start], F32, name="raw", tag="raw", bufs=4)
+            rows = weight[a * K_PASS : (a + 1) * K_PASS, cols]
+            nc.sync.dma_start(out=raw[:], in_=rows.rearrange("(p j) c -> p j c", j=PACK))
+            return raw
+
+        def load_tab(a):
+            nc.sync.dma_start(out=tab_t[a][:], in_=tab_words[a].rearrange("p t i -> p (t i)").bitcast(I32))
+
+        def load_quiet(b, t):
+            q = ring.tile([P, S], F32, name="q", tag="quiet", bufs=6)
+            rows = quiet[b * K_PASS : (b + 1) * K_PASS, :].rearrange("(p t) j -> p t j", t=PACK)
+            nc.sync.dma_start(out=q[:], in_=rows[:, t, :])
+            return q
+
+        def load_vec(vec, name):
+            v = keep.tile([P, R_PASSES, PACK], F32, name=name)
+            nc.scalar.dma_start(out=v[:], in_=vec.rearrange("(b p t) -> p b t", p=P, t=PACK))
+            return v
+
+        nc.vector.memset(tab_sc[:].bitcast(I32), 0)
+        nc.vector.memset(w3_sc[:].bitcast(I32), 0)
+        nc.sync.dma_start(offs_t[:], offs)
+        for quad in range(4):
+            nc.scalar.dma_start(
+                out=tab_sc[32 * quad : 32 * quad + 4 * K_PASSES, :].bitcast(I32),
+                in_=tab_scales[:, 4 * quad : 4 * quad + 4, :].bitcast(I32),
+            )
+        thr_t = load_vec(thr, "thr_t")
+        sharp_t = load_vec(sharp, "sharp_t")
+        share_t = load_vec(share, "share_t")
+        side_t = load_vec(side, "side_t")
+        for quad in range(4):
+            nc.gpsimd.dma_start(
+                out=w3_sc[32 * quad : 32 * quad + 4, :, :].bitcast(I32),
+                in_=w3_scales[:, 4 * quad : 4 * quad + 4, :].rearrange("b r n -> r b n").bitcast(I32),
+            )
+
+        w1_codes, w1_sc = {}, {}
+
+        def cast_w1(raw, eng):
+            bf = ring.tile([P, PACK * K_PASS], BF16, name="bf", tag="bf", bufs=3, align_bytes=64)
+            dst = bf[:].rearrange("p (t m j) -> p m j t", t=PACK, j=PACK)
+            src = raw[:].rearrange("p j (m t) -> p m j t", t=PACK)
+            if eng == "s":
+                nc.scalar.copy(out=dst, in_=src)
+            elif eng == "v":
+                nc.vector.tensor_copy(out=dst, in_=src)
+            else:
+                nc.gpsimd.tensor_scalar(out=dst, in0=src, scalar1=1.0, scalar2=0.0, op0=ALU.mult, op1=ALU.add)
+            return bf
+
+        def quant_w1(a, b, bf):
+            w1_codes[a, b] = keep.tile([P, K_PASS], U32, name="w1c%d%d" % (a, b), align_bytes=64)
+            w1_sc[a, b] = keep.tile([P, K_PASS], U8, name="w1s%d%d" % (a, b), align_bytes=64)
+            nc.vector.quantize_mx(out=w1_codes[a, b][:].bitcast(FP8X4), scales=w1_sc[a, b][:], in_=bf[:])
+
+        v_codes, v_sc = {}, {}
+
+        def gather_words(a):
+            for s in range(2):
+                v_codes[a, s] = keep.tile([P, BANK], U32, name="vc%d%d" % (a, s), align_bytes=64)
+                nc.vector.tensor_copy(
+                    v_codes[a, s][:], tab_t[a][:].bitcast(U32).indirect(offs_t[:, 32 * s : 32 * (s + 1)])
+                )
+
+        def gather_scales():
+            for s in range(2):
+                v_sc[s] = keep.tile([P, BANK], U8, name="vs%d" % s, align_bytes=64)
+                nc.vector.tensor_copy(v_sc[s][:], tab_sc[:].indirect(offs_t[:, 32 * s : 32 * (s + 1)]))
+
+        first = slice(0, K_PASS)
+        second = slice(K_PASS, 2 * K_PASS)
+        raw0 = load_raw(w1, 0, first)
+        load_tab(0)
+        raw1 = load_raw(w1, 1, first)
+        raw2 = load_raw(w1, 2, first)
+        nc.sync.dma_start(pos1_t[:], pos1)
+        nc.sync.dma_start(pos2_t[:], pos2)
+        load_tab(1)
+        load_tab(2)
+
+        gather_scales()
+        bf0 = cast_w1(raw0, "s")
+        gather_words(0)
+        quant_w1(0, 0, bf0)
+        bf1 = cast_w1(raw1, "s")
+        quant_w1(1, 0, bf1)
+        bf2 = cast_w1(raw2, "s")
+        gather_words(1)
+        quant_w1(2, 0, bf2)
+        gather_words(2)
+
+        slope = keep.tile([P, R_PASSES, PACK], F32, name="slope")
+        nc.gpsimd.tensor_tensor(out=slope[:], in0=sharp_t[:], in1=share_t[:], op=ALU.mult)
+        top = keep.tile([P, R_PASSES, PACK], F32, name="top")
+        c_bias = keep.tile([P, R_PASSES, PACK], F32, name="c_bias")
+
+        def scores(b, t, q):
+            h = ring.tile([P, S], F32, name="h", tag="h", bufs=5)
+            for s in range(2):
+                acc = psum.tile([P, BANK], F32, name="acc", tag="bank")
+                for a in range(K_PASSES):
+                    nc.tensor.matmul_mx(
+                        out=acc[:],
+                        lhsT=w1_codes[a, b][:, t * P : (t + 1) * P].bitcast(FP8X4),
+                        lhsT_scale=w1_sc[a, b][:, t * P : (t + 1) * P],
+                        rhs=v_codes[a, s][:].bitcast(FP8X4),
+                        rhs_scale=v_sc[s][4 * a : P, :],
+                        start=(a == 0),
+                        stop=(a == K_PASSES - 1),
+                    )
+                cols = slice(s * BANK, (s + 1) * BANK)
+                nc.vector.tensor_tensor(out=h[:, cols], in0=acc[:], in1=q[:, cols], op=ALU.max)
+            nc.vector.tensor_reduce(out=top[:, b, t : t + 1], in_=h[:], axis=AXIS.X, op=ALU.max)
+            nc.vector.tensor_scalar(
+                out=c_bias[:, b, t : t + 1], in0=top[:, b, t : t + 1], scalar1=slope[:, b, t : t + 1],
+                scalar2=-1.0, op0=ALU.mult, op1=ALU.mult,
+            )
+            return h
+
+        def looks(b, t, h, a_t, c_t, cols):
+            entries = slice(cols.start // 16, cols.stop // 16)
+            nc.scalar.activation(
+                out=a_t[:, t, :], in_=h[:].indirect(pos1_t[:, entries]), func=ACT.Sigmoid,
+                bias=thr_t[:, b, t : t + 1],
+            )
+            nc.scalar.activation(
+                out=c_t[:, t, :], in_=h[:].indirect(pos2_t[:, entries]), func=ACT.Sigmoid,
+                bias=c_bias[:, b, t : t + 1], scale=sharp_t[:, b, t : t + 1],
+            )
+
+        def contrast(b, t, a_t, c_t):
+            nc.gpsimd.tensor_tensor(out=a_t[:, t, :], in0=a_t[:, t, :], in1=c_t[:, t, :], op=ALU.subtract)
+
+        def scale(b, t, a_t, c_t):
+            nc.vector.tensor_scalar(
+                out=c_t[:, t, :], in0=a_t[:, t, :], scalar1=side_t[:, b, t : t + 1], scalar2=0.0,
+                op0=ALU.mult, op1=ALU.add,
+            )
+
+        def quant_d(d_t, width, name):
+            bf = keep.tile([P, width * PACK], BF16, name=name + "bf", align_bytes=64)
+            nc.vector.tensor_copy(
+                out=bf[:].rearrange("p (c i t) -> p c t i", i=4, t=PACK),
+                in_=d_t[:].rearrange("p t (c i) -> p c t i", i=4),
+            )
+            codes = keep.tile([P, width], U32, name=name + "c", align_bytes=64)
+            sc = keep.tile([P, width], U8, name=name + "s", align_bytes=64)
+            nc.vector.quantize_mx(out=codes[:].bitcast(FP8X4), scales=sc[:], in_=bf[:])
+            return codes, sc
+
+        a0 = keep.tile([P, PACK, M], F32, name="a0")
+        c0 = keep.tile([P, PACK, M], F32, name="c0")
+        a1 = [keep.tile([P, PACK, HALF], F32, name="a1%d" % u) for u in range(2)]
+        c1 = [keep.tile([P, PACK, HALF], F32, name="c1%d" % u) for u in range(2)]
+
+        w4_codes, w4_sc = {}, {}
+
+        def cast_w4(raw, eng):
+            bf = ring.tile([P, PACK * N], BF16, name="bf", tag="bf", bufs=3, align_bytes=64)
+            if eng == "s":
+                nc.scalar.copy(
+                    out=bf[:].rearrange("p (c i j) -> p c j i", i=4, j=PACK),
+                    in_=raw[:].rearrange("p j (c i) -> p c j i", i=4),
+                )
+            elif eng == "v":
+                nc.vector.tensor_copy(
+                    out=bf[:].rearrange("p (c i j) -> p c j i", i=4, j=PACK),
+                    in_=raw[:].rearrange("p j (c i) -> p c j i", i=4),
+                )
+            else:
+                nc.gpsimd.tensor_scalar(
+                    out=bf[:].rearrange("p (c j) -> p c j", j=PACK), in0=raw[:].rearrange("p j c -> p c j"),
+                    scalar1=1.0, scalar2=0.0, op0=ALU.mult, op1=ALU.add,
+                )
+            return bf
+
+        def quant_w4(b, bf):
+            w4_codes[b] = keep.tile([P, N], U32, name="w4c%d" % b, align_bytes=64)
+            w4_sc[b] = keep.tile([P, N], U8, name="w4s%d" % b, align_bytes=64)
+            for cols in (slice(0, 512), slice(512, N)):
+                nc.vector.quantize_mx(
+                    out=w4_codes[b][:, cols].bitcast(FP8X4), scales=w4_sc[b][:, cols],
+                    in_=bf[:, PACK * cols.start : PACK * cols.stop],
+                )
+
+        w1b1_eng = ["s","s","s"]
+        w4_eng = ["v","s"]
+        for t in range(PACK):
+            q = load_quiet(0, t)
+            h = scores(0, t, q)
+            looks(0, t, h, a0, c0, slice(0, M))
+            if t < K_PASSES:
+                raw = load_raw(w1, t, second)
+                quant_w1(t, 1, cast_w1(raw, w1b1_eng[t]))
+        for t in range(PACK):
+            contrast(0, t, a0, c0)
+
+
+        h1, raw4, bf4 = [], [], []
+        for t in range(PACK):
+            q = load_quiet(1, t)
+            if t % 2 == 0:
+                raw4.append(load_raw(w4, t // 2, slice(0, N)))
+            h1.append(scores(1, t, q))
+            looks(1, t, h1[t], a1[0], c1[0], slice(0, HALF))
+            if t % 2 == 1 and w4_eng[t // 2] == "g":
+                bf4.append(cast_w4(raw4[t // 2], "g"))
+            contrast(1, t, a1[0], c1[0])
+
+
+        nc.sync.dma_start(out=w3_t[:].bitcast(I32), in_=w3_words.rearrange("b p n -> p b n").bitcast(I32))
+        nc.sync.dma_start(out=duty_t[:], in_=duty.rearrange("(n p) m -> p n m", p=P))
+
+        for t in range(PACK):
+            looks(1, t, h1[t], a1[1], c1[1], slice(HALF, M))
+            contrast(1, t, a1[1], c1[1])
+
+        for t in range(PACK):
+            scale(0, t, a0, c0)
+
+        d0 = quant_d(c0, M, "d0")
+        for b in range(R_PASSES):
+            if w4_eng[b] != "g":
+                bf4.insert(b, cast_w4(raw4[b], w4_eng[b]))
+            quant_w4(b, bf4[b])
+        for t in range(PACK):
+            scale(1, t, a1[0], c1[0])
+
+        d1 = [quant_d(c1[0], HALF, "d10")]
+
+        def readings(u):
+            cols = slice(u * HALF, (u + 1) * HALF)
+            rhs = [d0[0][:, cols].bitcast(FP8X4), d1[u][0][:].bitcast(FP8X4)]
+            rhs_sc = [d0[1][:, cols], d1[u][1][:]]
+            for n in range(N_TILES):
+                ns = slice(n * P, (n + 1) * P)
+                acc = psum.tile([P, BANK], F32, name="acc", tag="bank")
+                for b in range(R_PASSES):
+                    nc.tensor.matmul_mx(
+                        out=acc[:, 0:HALF], lhsT=w3_t[:, b, 2 * n * P : 2 * (n + 1) * P].bitcast(FP4X4),
+                        lhsT_scale=w3_sc[:, b, ns], rhs=rhs[b], rhs_scale=rhs_sc[b],
+                        start=(b == 0), stop=(b == R_PASSES - 1),
+                    )
+                for b in range(R_PASSES):
+                    nc.tensor.matmul_mx(
+                        out=acc[:, HALF:BANK], lhsT=w4_codes[b][:, ns].bitcast(FP8X4),
+                        lhsT_scale=w4_sc[b][:, ns], rhs=rhs[b], rhs_scale=rhs_sc[b],
+                        start=(b == 0), stop=(b == R_PASSES - 1),
+                    )
+                alarm = ring.tile([P, HALF], F32, name="alarm", tag="alarm", bufs=4)
+                nc.scalar.activation(out=alarm[:], in_=acc[:, 0:HALF], func=ACT.Tanh)
+                (nc.vector if n % 2 == 0 and n > 0 else nc.gpsimd).tensor_tensor(out=alarm[:], in0=alarm[:], in1=duty_t[:, n, cols], op=ALU.mult)
+                res = ring.tile([P, HALF], F32, name="res", tag="res", bufs=5)
+                nc.vector.tensor_tensor(out=res[:], in0=acc[:, HALF:BANK], in1=alarm[:], op=ALU.add)
+                nc.sync.dma_start(out=out[ns, cols], in_=res[:])
+
+        readings(0)
+        for t in range(PACK):
+            scale(1, t, a1[1], c1[1])
+        d1.append(quant_d(c1[1], HALF, "d11"))
+        readings(1)

@@ -43,13 +43,12 @@ def tile_list_ammonia_leak_watch_kernel(
         pos2_t = lists.tile([P, M // 16], U16, name="pos2_t")
 
         tab_t = [keep.tile([P, T], I32, name="tab%d" % a, align_bytes=64) for a in range(K_PASSES)]
-        tab_sc = keep.tile([P, T], U8, name="tab_sc", align_bytes=64)
+        tab_sc = keep.tile([P, T], U8, name="tab_sc", tag="vc1", align_bytes=64)
         w3_sc = keep.tile([P, R_PASSES, N], U8, name="w3_sc", align_bytes=64)
         w3_t = keep.tile([P, R_PASSES, 2 * N], U8, name="w3_t", align_bytes=64)
-        duty_t = keep.tile([P, N_TILES, M], F32, name="duty_t")
 
         def load_raw(weight, a, cols):
-            raw = ring.tile([P, PACK, cols.stop - cols.start], F32, name="raw", tag="raw", bufs=4)
+            raw = ring.tile([P, PACK, cols.stop - cols.start], F32, name="raw", tag="raw", bufs=5)
             rows = weight[a * K_PASS : (a + 1) * K_PASS, cols]
             nc.sync.dma_start(out=raw[:], in_=rows.rearrange("(p j) c -> p j c", j=PACK))
             return raw
@@ -58,34 +57,22 @@ def tile_list_ammonia_leak_watch_kernel(
             nc.sync.dma_start(out=tab_t[a][:], in_=tab_words[a].rearrange("p t i -> p (t i)").bitcast(I32))
 
         def load_quiet(b, t):
-            q = ring.tile([P, S], F32, name="q", tag="quiet", bufs=6)
+            q = ring.tile([P, S], F32, name="q", tag="quiet%d" % ((PACK * b + t) % 6), align_bytes=64)
             rows = quiet[b * K_PASS : (b + 1) * K_PASS, :].rearrange("(p t) j -> p t j", t=PACK)
             nc.sync.dma_start(out=q[:], in_=rows[:, t, :])
             return q
 
-        def load_vec(vec, name):
+        def load_vec(vec, name, eng):
             v = keep.tile([P, R_PASSES, PACK], F32, name=name)
-            nc.scalar.dma_start(out=v[:], in_=vec.rearrange("(b p t) -> p b t", p=P, t=PACK))
+            eng.dma_start(out=v[:], in_=vec.rearrange("(b p t) -> p b t", p=P, t=PACK))
             return v
 
         nc.vector.memset(tab_sc[:].bitcast(I32), 0)
         nc.vector.memset(w3_sc[:].bitcast(I32), 0)
         nc.sync.dma_start(offs_t[:], offs)
-        for quad in range(4):
-            nc.scalar.dma_start(
-                out=tab_sc[32 * quad : 32 * quad + 4 * K_PASSES, :].bitcast(I32),
-                in_=tab_scales[:, 4 * quad : 4 * quad + 4, :].bitcast(I32),
-            )
-        thr_t = load_vec(thr, "thr_t")
-        sharp_t = load_vec(sharp, "sharp_t")
-        share_t = load_vec(share, "share_t")
-        side_t = load_vec(side, "side_t")
-        for quad in range(4):
-            nc.gpsimd.dma_start(
-                out=w3_sc[32 * quad : 32 * quad + 4, :, :].bitcast(I32),
-                in_=w3_scales[:, 4 * quad : 4 * quad + 4, :].rearrange("b r n -> r b n").bitcast(I32),
-            )
 
+        one = keep.tile([P, PACK], F32, name="one")
+        nc.gpsimd.memset(one[:], 1.0)
         w1_codes, w1_sc = {}, {}
 
         def cast_w1(raw, eng):
@@ -96,6 +83,12 @@ def tile_list_ammonia_leak_watch_kernel(
                 nc.scalar.copy(out=dst, in_=src)
             elif eng == "v":
                 nc.vector.tensor_copy(out=dst, in_=src)
+            elif eng == "t":
+                dst = bf[:].rearrange("p (t m j) -> p t m j", t=PACK, j=PACK)
+                src = raw[:].rearrange("p j (m t) -> p t m j", t=PACK)
+                ones = one[:].unsqueeze(1).to_broadcast([P, P, PACK])
+                for t in range(PACK):
+                    nc.gpsimd.tensor_tensor(out=dst[:, t], in0=src[:, t], in1=ones, op=ALU.mult)
             else:
                 nc.gpsimd.tensor_scalar(out=dst, in0=src, scalar1=1.0, scalar2=0.0, op0=ALU.mult, op1=ALU.add)
             return bf
@@ -108,8 +101,9 @@ def tile_list_ammonia_leak_watch_kernel(
         v_codes, v_sc = {}, {}
 
         def gather_words(a):
+            both = keep.tile([P, S], U32, name="vc%d" % a, align_bytes=64)
             for s in range(2):
-                v_codes[a, s] = keep.tile([P, BANK], U32, name="vc%d%d" % (a, s), align_bytes=64)
+                v_codes[a, s] = both[:, s * BANK : (s + 1) * BANK]
                 nc.vector.tensor_copy(
                     v_codes[a, s][:], tab_t[a][:].bitcast(U32).indirect(offs_t[:, 32 * s : 32 * (s + 1)])
                 )
@@ -122,12 +116,20 @@ def tile_list_ammonia_leak_watch_kernel(
         first = slice(0, K_PASS)
         second = slice(K_PASS, 2 * K_PASS)
         raw0 = load_raw(w1, 0, first)
+        for quad in range(4):
+            nc.sync.dma_start(
+                out=tab_sc[32 * quad : 32 * quad + 4 * K_PASSES, :].bitcast(I32),
+                in_=tab_scales[:, 4 * quad : 4 * quad + 4, :].bitcast(I32),
+            )
         load_tab(0)
         raw1 = load_raw(w1, 1, first)
         raw2 = load_raw(w1, 2, first)
+        load_tab(1)
         nc.sync.dma_start(pos1_t[:], pos1)
         nc.sync.dma_start(pos2_t[:], pos2)
-        load_tab(1)
+        sharp_t = load_vec(sharp, "sharp_t", nc.sync)
+        share_t = load_vec(share, "share_t", nc.sync)
+        thr_t = load_vec(thr, "thr_t", nc.sync)
         load_tab(2)
 
         gather_scales()
@@ -147,7 +149,7 @@ def tile_list_ammonia_leak_watch_kernel(
         c_bias = keep.tile([P, R_PASSES, PACK], F32, name="c_bias")
 
         def scores(b, t, q):
-            h = ring.tile([P, S], F32, name="h", tag="h", bufs=5)
+            h = ring.tile([P, S], F32, name="h", tag="h%d%d" % (b, t), align_bytes=64)
             for s in range(2):
                 acc = psum.tile([P, BANK], F32, name="acc", tag="bank")
                 for a in range(K_PASSES):
@@ -180,35 +182,53 @@ def tile_list_ammonia_leak_watch_kernel(
                 bias=c_bias[:, b, t : t + 1], scale=sharp_t[:, b, t : t + 1],
             )
 
-        def contrast(b, t, a_t, c_t):
+        def contrast(t, a_t, c_t):
             nc.gpsimd.tensor_tensor(out=a_t[:, t, :], in0=a_t[:, t, :], in1=c_t[:, t, :], op=ALU.subtract)
 
-        def scale(b, t, a_t, c_t):
-            nc.vector.tensor_scalar(
-                out=c_t[:, t, :], in0=a_t[:, t, :], scalar1=side_t[:, b, t : t + 1], scalar2=0.0,
+        def scale(eng, b, t, a_t, d_t):
+            eng.tensor_scalar(
+                out=d_t[:, t, :], in0=a_t[:, t, :], scalar1=side_t[:, b, t : t + 1], scalar2=0.0,
                 op0=ALU.mult, op1=ALU.add,
             )
 
-        def quant_d(d_t, width, name):
-            bf = keep.tile([P, width * PACK], BF16, name=name + "bf", align_bytes=64)
-            nc.vector.tensor_copy(
-                out=bf[:].rearrange("p (c i t) -> p c t i", i=4, t=PACK),
-                in_=d_t[:].rearrange("p t (c i) -> p c t i", i=4),
-            )
+        def quant_d(b, a_t, c_t, width, name, how, tag):
+            bf = ring.tile([P, width * PACK], BF16, name=name + "bf", tag=tag, align_bytes=64)
+            dst = bf[:].rearrange("p (c i t) -> p c t i", i=4, t=PACK)
+            if how == "fused":
+                step = 32
+                for c in range(0, width // 4, step):
+                    nc.vector.tensor_tensor(
+                        out=dst[:, c : c + step], in0=a_t[:].rearrange("p t (c i) -> p c t i", i=4)[:, c : c + step],
+                        in1=side_t[:, b, :].unsqueeze(1).unsqueeze(3).to_broadcast([P, step, PACK, 4]),
+                        op=ALU.mult,
+                    )
+            elif how == "fg":
+                step = 128
+                for c in range(0, width, step):
+                    nc.gpsimd.tensor_tensor(
+                        out=bf[:].rearrange("p (m t) -> p m t", t=PACK)[:, c : c + step],
+                        in0=a_t[:].rearrange("p t m -> p m t")[:, c : c + step],
+                        in1=side_t[:, b, :].unsqueeze(1).to_broadcast([P, step, PACK]), op=ALU.mult,
+                    )
+            else:
+                if how[0] == "v":
+                    c_t = ring.tile([P, PACK, width], BF16, name=name + "ds", tag={"d0":"quiet1","d10":"quiet4","d11":"h00"}[name], align_bytes=64)
+                    for t in range(PACK):
+                        scale(nc.vector, b, t, a_t, c_t)
+                src = c_t[:].rearrange("p t (c i) -> p c t i", i=4)
+                if how[1] == "s":
+                    nc.scalar.copy(out=dst, in_=src)
+                else:
+                    nc.vector.tensor_copy(out=dst, in_=src)
             codes = keep.tile([P, width], U32, name=name + "c", align_bytes=64)
             sc = keep.tile([P, width], U8, name=name + "s", align_bytes=64)
             nc.vector.quantize_mx(out=codes[:].bitcast(FP8X4), scales=sc[:], in_=bf[:])
             return codes, sc
 
-        a0 = keep.tile([P, PACK, M], F32, name="a0")
-        c0 = keep.tile([P, PACK, M], F32, name="c0")
-        a1 = [keep.tile([P, PACK, HALF], F32, name="a1%d" % u) for u in range(2)]
-        c1 = [keep.tile([P, PACK, HALF], F32, name="c1%d" % u) for u in range(2)]
-
         w4_codes, w4_sc = {}, {}
 
-        def cast_w4(raw, eng):
-            bf = ring.tile([P, PACK * N], BF16, name="bf", tag="bf", bufs=3, align_bytes=64)
+        def cast_w4(raw, eng, tag):
+            bf = ring.tile([P, PACK * N], BF16, name="bf", tag=tag, align_bytes=64)
             if eng == "s":
                 nc.scalar.copy(
                     out=bf[:].rearrange("p (c i j) -> p c j i", i=4, j=PACK),
@@ -219,6 +239,14 @@ def tile_list_ammonia_leak_watch_kernel(
                     out=bf[:].rearrange("p (c i j) -> p c j i", i=4, j=PACK),
                     in_=raw[:].rearrange("p j (c i) -> p c j i", i=4),
                 )
+            elif eng == "t":
+                for m in range(0, N, P):
+                    ms = slice(m, m + P)
+                    nc.gpsimd.tensor_tensor(
+                        out=bf[:].rearrange("p (c j) -> p c j", j=PACK)[:, ms],
+                        in0=raw[:].rearrange("p j c -> p c j")[:, ms],
+                        in1=one[:].unsqueeze(1).to_broadcast([P, P, PACK]), op=ALU.mult,
+                    )
             else:
                 nc.gpsimd.tensor_scalar(
                     out=bf[:].rearrange("p (c j) -> p c j", j=PACK), in0=raw[:].rearrange("p j c -> p c j"),
@@ -227,7 +255,7 @@ def tile_list_ammonia_leak_watch_kernel(
             return bf
 
         def quant_w4(b, bf):
-            w4_codes[b] = keep.tile([P, N], U32, name="w4c%d" % b, align_bytes=64)
+            w4_codes[b] = ring.tile([P, N], U32, name="w4c%d" % b, tag=["quiet5","quiet0"][b], align_bytes=64)
             w4_sc[b] = keep.tile([P, N], U8, name="w4s%d" % b, align_bytes=64)
             for cols in (slice(0, 512), slice(512, N)):
                 nc.vector.quantize_mx(
@@ -235,50 +263,70 @@ def tile_list_ammonia_leak_watch_kernel(
                     in_=bf[:, PACK * cols.start : PACK * cols.stop],
                 )
 
-        w1b1_eng = ["s","s","s"]
-        w4_eng = ["v","s"]
-        for t in range(PACK):
-            q = load_quiet(0, t)
-            h = scores(0, t, q)
-            looks(0, t, h, a0, c0, slice(0, M))
-            if t < K_PASSES:
-                raw = load_raw(w1, t, second)
-                quant_w1(t, 1, cast_w1(raw, w1b1_eng[t]))
-        for t in range(PACK):
-            contrast(0, t, a0, c0)
 
-
-        h1, raw4, bf4 = [], [], []
+        w1b1_eng = ["t","t","v"]
+        w4_eng = ["s","t"]
+        duty_eng = ["gvgvg","gvgvg"]
+        how = ["vv","vv","vv"]
+        side_t = load_vec(side, "side_t", nc.sync)
+        qs, raws = {}, {}
+        for item in ["q00","q01","w0","q02","w1","q03","w2","x0","q10","x1","q11","q12","q13"]:
+            if item[0] == "q":
+                qs[int(item[1]), int(item[2])] = load_quiet(int(item[1]), int(item[2]))
+            elif item[0] == "w":
+                raws[int(item[1])] = load_raw(w1, int(item[1]), second)
+            elif item[0] == "x":
+                raws[item] = load_raw(w4, int(item[1]), slice(0, N))
+        bf_b1 = {a: cast_w1(raws[a], w1b1_eng[a]) for a in range(K_PASSES) if w1b1_eng[a] != "v"}
+        h0 = []
+        vcast = [3,3,3]
         for t in range(PACK):
-            q = load_quiet(1, t)
-            if t % 2 == 0:
-                raw4.append(load_raw(w4, t // 2, slice(0, N)))
+            h0.append(scores(0, t, qs[0, t]))
+            for a in range(K_PASSES):
+                if vcast[a] == t:
+                    if w1b1_eng[a] == "v":
+                        bf_b1[a] = cast_w1(raws[a], "v")
+                    quant_w1(a, 1, bf_b1[a])
+        a0 = ring.tile([P, PACK, M], F32, name="a0", tag="a0")
+        c0 = ring.tile([P, PACK, M], F32, name="c0", tag="c0")
+        a1 = [keep.tile([P, PACK, HALF], F32, name="a1%d" % u) for u in range(2)]
+        c1 = [keep.tile([P, PACK, HALF], F32, name="c1%d" % u) for u in range(2)]
+        for t in range(PACK):
+            looks(0, t, h0[t], a0, c0, slice(0, M))
+            contrast(t, a0, c0)
+            if how[0][0] == "g":
+                scale(nc.gpsimd, 0, t, a0, c0)
+
+        raw4, bf4 = [raws["x0"], raws["x1"]], {}
+        w4_load, w4_cast = [0,1], [9,0]
+        h1 = []
+        for t in range(PACK):
+            q = qs[1, t]
+            if t in w4_cast:
+                b = w4_cast.index(t)
+                bf4[b] = cast_w4(raw4[b], w4_eng[b], ["h03","bf4"][b])
             h1.append(scores(1, t, q))
-            looks(1, t, h1[t], a1[0], c1[0], slice(0, HALF))
-            if t % 2 == 1 and w4_eng[t // 2] == "g":
-                bf4.append(cast_w4(raw4[t // 2], "g"))
-            contrast(1, t, a1[0], c1[0])
-
-
+            for u in range(2):
+                looks(1, t, h1[t], a1[u], c1[u], slice(u * HALF, (u + 1) * HALF))
+                contrast(t, a1[u], c1[u])
+                if how[1 + u][0] == "g":
+                    scale(nc.gpsimd, 1, t, a1[u], c1[u])
+        for quad in range(4):
+            nc.sync.dma_start(
+                out=w3_sc[32 * quad : 32 * quad + 4, :, :].bitcast(I32),
+                in_=w3_scales[:, 4 * quad : 4 * quad + 4, :].rearrange("b r n -> r b n").bitcast(I32),
+            )
         nc.sync.dma_start(out=w3_t[:].bitcast(I32), in_=w3_words.rearrange("b p n -> p b n").bitcast(I32))
+        duty_t = ring.tile([P, N_TILES, M], F32, name="duty_t", tag="raw", bufs=5)
         nc.sync.dma_start(out=duty_t[:], in_=duty.rearrange("(n p) m -> p n m", p=P))
 
-        for t in range(PACK):
-            looks(1, t, h1[t], a1[1], c1[1], slice(HALF, M))
-            contrast(1, t, a1[1], c1[1])
 
-        for t in range(PACK):
-            scale(0, t, a0, c0)
-
-        d0 = quant_d(c0, M, "d0")
+        d0 = quant_d(0, a0, c0, M, "d0", how[0], "h01")
         for b in range(R_PASSES):
-            if w4_eng[b] != "g":
-                bf4.insert(b, cast_w4(raw4[b], w4_eng[b]))
+            if b not in bf4:
+                bf4[b] = cast_w4(raw4[b], w4_eng[b], ["h03","bf4"][b])
             quant_w4(b, bf4[b])
-        for t in range(PACK):
-            scale(1, t, a1[0], c1[0])
-
-        d1 = [quant_d(c1[0], HALF, "d10")]
+        d1 = [quant_d(1, a1[0], c1[0], HALF, "d10", how[1], "quiet2")]
 
         def readings(u):
             cols = slice(u * HALF, (u + 1) * HALF)
@@ -301,13 +349,12 @@ def tile_list_ammonia_leak_watch_kernel(
                     )
                 alarm = ring.tile([P, HALF], F32, name="alarm", tag="alarm", bufs=4)
                 nc.scalar.activation(out=alarm[:], in_=acc[:, 0:HALF], func=ACT.Tanh)
-                (nc.vector if n % 2 == 0 and n > 0 else nc.gpsimd).tensor_tensor(out=alarm[:], in0=alarm[:], in1=duty_t[:, n, cols], op=ALU.mult)
+                (nc.gpsimd if duty_eng[u][n] == "g" else nc.vector).tensor_tensor(out=alarm[:], in0=alarm[:], in1=duty_t[:, n, cols], op=ALU.mult)
                 res = ring.tile([P, HALF], F32, name="res", tag="res", bufs=5)
                 nc.vector.tensor_tensor(out=res[:], in0=acc[:, HALF:BANK], in1=alarm[:], op=ALU.add)
                 nc.sync.dma_start(out=out[ns, cols], in_=res[:])
 
+
         readings(0)
-        for t in range(PACK):
-            scale(1, t, a1[1], c1[1])
-        d1.append(quant_d(c1[1], HALF, "d11"))
+        d1.append(quant_d(1, a1[1], c1[1], HALF, "d11", how[2], "quiet3"))
         readings(1)

@@ -47,8 +47,8 @@ def tile_list_ammonia_leak_watch_kernel(
         w3_sc = keep.tile([P, R_PASSES, N], U8, name="w3_sc", align_bytes=64)
         w3_t = keep.tile([P, R_PASSES, 2 * N], U8, name="w3_t", align_bytes=64)
 
-        def load_raw(weight, a, cols):
-            raw = ring.tile([P, PACK, cols.stop - cols.start], F32, name="raw", tag="raw", bufs=5)
+        def load_raw(weight, a, cols, tag):
+            raw = ring.tile([P, PACK, cols.stop - cols.start], F32, name="raw", tag=tag)
             rows = weight[a * K_PASS : (a + 1) * K_PASS, cols]
             nc.sync.dma_start(out=raw[:], in_=rows.rearrange("(p j) c -> p j c", j=PACK))
             return raw
@@ -57,55 +57,55 @@ def tile_list_ammonia_leak_watch_kernel(
             nc.sync.dma_start(out=tab_t[a][:], in_=tab_words[a].rearrange("p t i -> p (t i)").bitcast(I32))
 
         def load_quiet(b, t):
-            q = ring.tile([P, S], F32, name="q", tag="quiet%d" % ((PACK * b + t) % 6), align_bytes=64)
+            q = ring.tile([P, S], F32, name="q", tag="q%d%d" % (b, t), align_bytes=64)
             rows = quiet[b * K_PASS : (b + 1) * K_PASS, :].rearrange("(p t) j -> p t j", t=PACK)
             nc.sync.dma_start(out=q[:], in_=rows[:, t, :])
             return q
 
-        def load_vec(vec, name, eng):
+        def load_vec(vec, name):
             v = keep.tile([P, R_PASSES, PACK], F32, name=name)
-            eng.dma_start(out=v[:], in_=vec.rearrange("(b p t) -> p b t", p=P, t=PACK))
+            nc.sync.dma_start(out=v[:], in_=vec.rearrange("(b p t) -> p b t", p=P, t=PACK))
             return v
 
-        nc.vector.memset(tab_sc[:].bitcast(I32), 0)
+        nc.gpsimd.memset(tab_sc[:].bitcast(I32), 0)
         nc.vector.memset(w3_sc[:].bitcast(I32), 0)
         nc.sync.dma_start(offs_t[:], offs)
+        for quad in range(4):
+            nc.gpsimd.dma_start(
+                out=tab_sc[32 * quad : 32 * quad + 4 * K_PASSES, :].bitcast(I32),
+                in_=tab_scales[:, 4 * quad : 4 * quad + 4, :].bitcast(I32),
+            )
 
-        one = keep.tile([P, PACK], F32, name="one")
-        nc.gpsimd.memset(one[:], 1.0)
+        def copy_on(eng, out, in_):
+            if eng == "s":
+                nc.scalar.copy(out=out, in_=in_)
+            else:
+                nc.vector.tensor_copy(out=out, in_=in_)
+
         w1_codes, w1_sc = {}, {}
 
-        def cast_w1(raw, eng):
-            bf = ring.tile([P, PACK * K_PASS], BF16, name="bf", tag="bf", bufs=3, align_bytes=64)
-            dst = bf[:].rearrange("p (t m j) -> p m j t", t=PACK, j=PACK)
-            src = raw[:].rearrange("p j (m t) -> p m j t", t=PACK)
-            if eng == "s":
-                nc.scalar.copy(out=dst, in_=src)
-            elif eng == "v":
-                nc.vector.tensor_copy(out=dst, in_=src)
-            elif eng == "t":
-                dst = bf[:].rearrange("p (t m j) -> p t m j", t=PACK, j=PACK)
-                src = raw[:].rearrange("p j (m t) -> p t m j", t=PACK)
-                ones = one[:].unsqueeze(1).to_broadcast([P, P, PACK])
-                for t in range(PACK):
-                    nc.gpsimd.tensor_tensor(out=dst[:, t], in0=src[:, t], in1=ones, op=ALU.mult)
-            else:
-                nc.gpsimd.tensor_scalar(out=dst, in0=src, scalar1=1.0, scalar2=0.0, op0=ALU.mult, op1=ALU.add)
+        def cast_w1(raw, eng, tag):
+            bf = ring.tile([P, PACK * K_PASS], BF16, name="bf", tag=tag, align_bytes=64)
+            copy_on(
+                eng,
+                bf[:].rearrange("p (t m j) -> p m j t", t=PACK, j=PACK),
+                raw[:].rearrange("p j (m t) -> p m j t", t=PACK),
+            )
             return bf
 
         def quant_w1(a, b, bf):
-            w1_codes[a, b] = keep.tile([P, K_PASS], U32, name="w1c%d%d" % (a, b), align_bytes=64)
+            w1_codes[a, b] = ring.tile([P, K_PASS], U32, name="w1c%d%d" % (a, b), tag={}.get("%d%d" % (a, b), "w1c%d%d" % (a, b)), align_bytes=64)
             w1_sc[a, b] = keep.tile([P, K_PASS], U8, name="w1s%d%d" % (a, b), align_bytes=64)
             nc.vector.quantize_mx(out=w1_codes[a, b][:].bitcast(FP8X4), scales=w1_sc[a, b][:], in_=bf[:])
 
         v_codes, v_sc = {}, {}
 
         def gather_words(a):
-            both = keep.tile([P, S], U32, name="vc%d" % a, align_bytes=64)
+            v_codes[a] = keep.tile([P, S], U32, name="vc%d" % a, align_bytes=64)
             for s in range(2):
-                v_codes[a, s] = both[:, s * BANK : (s + 1) * BANK]
                 nc.vector.tensor_copy(
-                    v_codes[a, s][:], tab_t[a][:].bitcast(U32).indirect(offs_t[:, 32 * s : 32 * (s + 1)])
+                    v_codes[a][:, s * BANK : (s + 1) * BANK],
+                    tab_t[a][:].bitcast(U32).indirect(offs_t[:, 32 * s : 32 * (s + 1)]),
                 )
 
         def gather_scales():
@@ -115,30 +115,26 @@ def tile_list_ammonia_leak_watch_kernel(
 
         first = slice(0, K_PASS)
         second = slice(K_PASS, 2 * K_PASS)
-        raw0 = load_raw(w1, 0, first)
-        for quad in range(4):
-            nc.sync.dma_start(
-                out=tab_sc[32 * quad : 32 * quad + 4 * K_PASSES, :].bitcast(I32),
-                in_=tab_scales[:, 4 * quad : 4 * quad + 4, :].bitcast(I32),
-            )
+        raw0 = load_raw(w1, 0, first, "r0")
         load_tab(0)
-        raw1 = load_raw(w1, 1, first)
-        raw2 = load_raw(w1, 2, first)
+        raw1 = load_raw(w1, 1, first, "r1")
+        raw2 = load_raw(w1, 2, first, "r2")
         load_tab(1)
         nc.sync.dma_start(pos1_t[:], pos1)
         nc.sync.dma_start(pos2_t[:], pos2)
-        sharp_t = load_vec(sharp, "sharp_t", nc.sync)
-        share_t = load_vec(share, "share_t", nc.sync)
-        thr_t = load_vec(thr, "thr_t", nc.sync)
+        sharp_t = load_vec(sharp, "sharp_t")
+        share_t = load_vec(share, "share_t")
+        thr_t = load_vec(thr, "thr_t")
         load_tab(2)
+        side_t = load_vec(side, "side_t")
 
         gather_scales()
-        bf0 = cast_w1(raw0, "s")
+        bf0 = cast_w1(raw0, "s", "bf0")
         gather_words(0)
         quant_w1(0, 0, bf0)
-        bf1 = cast_w1(raw1, "s")
+        bf1 = cast_w1(raw1, "s", "bf1")
         quant_w1(1, 0, bf1)
-        bf2 = cast_w1(raw2, "s")
+        bf2 = cast_w1(raw2, "s", "bf2")
         gather_words(1)
         quant_w1(2, 0, bf2)
         gather_words(2)
@@ -150,19 +146,20 @@ def tile_list_ammonia_leak_watch_kernel(
 
         def scores(b, t, q):
             h = ring.tile([P, S], F32, name="h", tag="h%d%d" % (b, t), align_bytes=64)
+            order = [0,1,2] if b else [0, 1, 2]
             for s in range(2):
+                cols = slice(s * BANK, (s + 1) * BANK)
                 acc = psum.tile([P, BANK], F32, name="acc", tag="bank")
-                for a in range(K_PASSES):
+                for a in order:
                     nc.tensor.matmul_mx(
                         out=acc[:],
                         lhsT=w1_codes[a, b][:, t * P : (t + 1) * P].bitcast(FP8X4),
                         lhsT_scale=w1_sc[a, b][:, t * P : (t + 1) * P],
-                        rhs=v_codes[a, s][:].bitcast(FP8X4),
+                        rhs=v_codes[a][:, cols].bitcast(FP8X4),
                         rhs_scale=v_sc[s][4 * a : P, :],
-                        start=(a == 0),
-                        stop=(a == K_PASSES - 1),
+                        start=(a == order[0]),
+                        stop=(a == order[-1]),
                     )
-                cols = slice(s * BANK, (s + 1) * BANK)
                 nc.vector.tensor_tensor(out=h[:, cols], in0=acc[:], in1=q[:, cols], op=ALU.max)
             nc.vector.tensor_reduce(out=top[:, b, t : t + 1], in_=h[:], axis=AXIS.X, op=ALU.max)
             nc.vector.tensor_scalar(
@@ -171,190 +168,189 @@ def tile_list_ammonia_leak_watch_kernel(
             )
             return h
 
-        def looks(b, t, h, a_t, c_t, cols):
+        def looks(b, t, h, piece, cols):
             entries = slice(cols.start // 16, cols.stop // 16)
             nc.scalar.activation(
-                out=a_t[:, t, :], in_=h[:].indirect(pos1_t[:, entries]), func=ACT.Sigmoid,
+                out=a_t[piece][:, t, :], in_=h[:].indirect(pos1_t[:, entries]), func=ACT.Sigmoid,
                 bias=thr_t[:, b, t : t + 1],
             )
             nc.scalar.activation(
-                out=c_t[:, t, :], in_=h[:].indirect(pos2_t[:, entries]), func=ACT.Sigmoid,
+                out=c_t[piece][:, t, :], in_=h[:].indirect(pos2_t[:, entries]), func=ACT.Sigmoid,
                 bias=c_bias[:, b, t : t + 1], scale=sharp_t[:, b, t : t + 1],
             )
 
-        def contrast(t, a_t, c_t):
-            nc.gpsimd.tensor_tensor(out=a_t[:, t, :], in0=a_t[:, t, :], in1=c_t[:, t, :], op=ALU.subtract)
+        diff_eng = {"d0":"gggg","d10":"vvvv","d11":"vvvv"}
+        how = {"d0":"vv","d10":"vv","d11":"sv"}
+        tags = {"w0":"r3","w1":"r0","w2":"r1","x0":"r2","x1":"r3","duty":"r0","gd0":"bf2","sd0":"q13","id0":"h01","vd0":"r1","vd10":"q01","vd11":"q00","sd10":"q10","sd11":"h00","id10":"q02","id11":"q03","bf40":"h02","bf41":"h13","w4c0":"q11","w4c1":"q12"}
+        width = {"d0": M, "d10": HALF, "d11": HALF}
+        a_t, c_t, dd_g, dd_v = {}, {}, {}, {}
 
-        def scale(eng, b, t, a_t, d_t):
-            eng.tensor_scalar(
-                out=d_t[:, t, :], in0=a_t[:, t, :], scalar1=side_t[:, b, t : t + 1], scalar2=0.0,
-                op0=ALU.mult, op1=ALU.add,
-            )
+        def look_tiles(piece):
+            a_t[piece] = ring.tile([P, PACK, width[piece]], F32, name="a" + piece, tag=tags.get("a" + piece, "a" + piece), align_bytes=64)
+            c_t[piece] = ring.tile([P, PACK, width[piece]], F32, name="c" + piece, tag=tags.get("c" + piece, "c" + piece), align_bytes=64)
 
-        def quant_d(b, a_t, c_t, width, name, how, tag):
-            bf = ring.tile([P, width * PACK], BF16, name=name + "bf", tag=tag, align_bytes=64)
-            dst = bf[:].rearrange("p (c i t) -> p c t i", i=4, t=PACK)
-            if how == "fused":
-                step = 32
-                for c in range(0, width // 4, step):
-                    nc.vector.tensor_tensor(
-                        out=dst[:, c : c + step], in0=a_t[:].rearrange("p t (c i) -> p c t i", i=4)[:, c : c + step],
-                        in1=side_t[:, b, :].unsqueeze(1).unsqueeze(3).to_broadcast([P, step, PACK, 4]),
-                        op=ALU.mult,
+        def diff_on_gpsimd(piece, t):
+            if diff_eng[piece][t] == "g":
+                if piece not in dd_g:
+                    if "g" + piece in tags:
+                        dd_g[piece] = ring.tile([P, PACK, width[piece]], F32, name="g" + piece, tag=tags["g" + piece], align_bytes=64)
+                    else:
+                        dd_g[piece] = a_t[piece]
+                nc.gpsimd.tensor_tensor(
+                    out=dd_g[piece][:, t, :], in0=a_t[piece][:, t, :], in1=c_t[piece][:, t, :], op=ALU.subtract
+                )
+
+        def diff_on_vector(piece):
+            w = width[piece]
+            first_v = (list(diff_eng[piece]) + ["v"]).index("v") if "v" in diff_eng[piece] else -1
+            if first_v >= 0:
+                dd = ring.tile([P, PACK - first_v, w], F32, name="v" + piece, tag=tags["v" + piece], align_bytes=64)
+                nc.vector.tensor_tensor(
+                    out=dd[:], in0=a_t[piece][:, first_v:PACK, :], in1=c_t[piece][:, first_v:PACK, :], op=ALU.subtract
+                )
+                dd_v[piece] = dd
+
+        def quant_d(b, piece):
+            w = width[piece]
+            first_v = (list(diff_eng[piece]) + ["v"]).index("v") if "v" in diff_eng[piece] else -1
+            dd = dd_v.get(piece)
+            ds = ring.tile([P, PACK, w], BF16, name="s" + piece, tag=tags["s" + piece], align_bytes=64)
+            for t in range(PACK):
+                diff = dd[:, t - first_v, :] if 0 <= first_v <= t else dd_g[piece][:, t, :]
+                if how[piece][0] == "v":
+                    nc.vector.tensor_scalar(
+                        out=ds[:, t, :], in0=diff, scalar1=side_t[:, b, t : t + 1], scalar2=None, op0=ALU.mult
                     )
-            elif how == "fg":
-                step = 128
-                for c in range(0, width, step):
-                    nc.gpsimd.tensor_tensor(
-                        out=bf[:].rearrange("p (m t) -> p m t", t=PACK)[:, c : c + step],
-                        in0=a_t[:].rearrange("p t m -> p m t")[:, c : c + step],
-                        in1=side_t[:, b, :].unsqueeze(1).to_broadcast([P, step, PACK]), op=ALU.mult,
-                    )
-            else:
-                if how[0] == "v":
-                    c_t = ring.tile([P, PACK, width], BF16, name=name + "ds", tag={"d0":"quiet1","d10":"quiet4","d11":"h00"}[name], align_bytes=64)
-                    for t in range(PACK):
-                        scale(nc.vector, b, t, a_t, c_t)
-                src = c_t[:].rearrange("p t (c i) -> p c t i", i=4)
-                if how[1] == "s":
-                    nc.scalar.copy(out=dst, in_=src)
                 else:
-                    nc.vector.tensor_copy(out=dst, in_=src)
-            codes = keep.tile([P, width], U32, name=name + "c", align_bytes=64)
-            sc = keep.tile([P, width], U8, name=name + "s", align_bytes=64)
+                    nc.scalar.activation(out=ds[:, t, :], in_=diff, func=ACT.Copy, scale=side_t[:, b, t : t + 1])
+            bf = ring.tile([P, w * PACK], BF16, name="i" + piece, tag=tags["i" + piece], align_bytes=64)
+            copy_on(
+                how[piece][1],
+                bf[:].rearrange("p (c i t) -> p c t i", i=4, t=PACK),
+                ds[:].rearrange("p t (c i) -> p c t i", i=4),
+            )
+            codes = ring.tile([P, w], U32, name="q" + piece, tag=tags.get("q" + piece, "q" + piece), align_bytes=64)
+            sc = keep.tile([P, w], U8, name=piece + "s", align_bytes=64)
             nc.vector.quantize_mx(out=codes[:].bitcast(FP8X4), scales=sc[:], in_=bf[:])
             return codes, sc
 
-        w4_codes, w4_sc = {}, {}
+        w4_codes, w4_sc, bf4 = {}, {}, {}
+        w4_eng = ["s","s"]
 
-        def cast_w4(raw, eng, tag):
-            bf = ring.tile([P, PACK * N], BF16, name="bf", tag=tag, align_bytes=64)
-            if eng == "s":
-                nc.scalar.copy(
-                    out=bf[:].rearrange("p (c i j) -> p c j i", i=4, j=PACK),
-                    in_=raw[:].rearrange("p j (c i) -> p c j i", i=4),
-                )
-            elif eng == "v":
-                nc.vector.tensor_copy(
-                    out=bf[:].rearrange("p (c i j) -> p c j i", i=4, j=PACK),
-                    in_=raw[:].rearrange("p j (c i) -> p c j i", i=4),
-                )
-            elif eng == "t":
-                for m in range(0, N, P):
-                    ms = slice(m, m + P)
-                    nc.gpsimd.tensor_tensor(
-                        out=bf[:].rearrange("p (c j) -> p c j", j=PACK)[:, ms],
-                        in0=raw[:].rearrange("p j c -> p c j")[:, ms],
-                        in1=one[:].unsqueeze(1).to_broadcast([P, P, PACK]), op=ALU.mult,
-                    )
-            else:
-                nc.gpsimd.tensor_scalar(
-                    out=bf[:].rearrange("p (c j) -> p c j", j=PACK), in0=raw[:].rearrange("p j c -> p c j"),
-                    scalar1=1.0, scalar2=0.0, op0=ALU.mult, op1=ALU.add,
-                )
-            return bf
+        def cast_w4(b):
+            bf4[b] = ring.tile([P, PACK * N], BF16, name="bf4", tag=tags["bf4%d" % b], align_bytes=64)
+            copy_on(
+                w4_eng[b],
+                bf4[b][:].rearrange("p (c i j) -> p c j i", i=4, j=PACK),
+                raws["x%d" % b][:].rearrange("p j (c i) -> p c j i", i=4),
+            )
 
-        def quant_w4(b, bf):
-            w4_codes[b] = ring.tile([P, N], U32, name="w4c%d" % b, tag=["quiet5","quiet0"][b], align_bytes=64)
+        def quant_w4(b):
+            w4_codes[b] = ring.tile([P, N], U32, name="w4c%d" % b, tag=tags["w4c%d" % b], align_bytes=64)
             w4_sc[b] = keep.tile([P, N], U8, name="w4s%d" % b, align_bytes=64)
             for cols in (slice(0, 512), slice(512, N)):
                 nc.vector.quantize_mx(
                     out=w4_codes[b][:, cols].bitcast(FP8X4), scales=w4_sc[b][:, cols],
-                    in_=bf[:, PACK * cols.start : PACK * cols.stop],
+                    in_=bf4[b][:, PACK * cols.start : PACK * cols.stop],
                 )
 
-
-        w1b1_eng = ["t","t","v"]
-        w4_eng = ["s","t"]
-        duty_eng = ["gvgvg","gvgvg"]
-        how = ["vv","vv","vv"]
-        side_t = load_vec(side, "side_t", nc.sync)
         qs, raws = {}, {}
         for item in ["q00","q01","w0","q02","w1","q03","w2","x0","q10","x1","q11","q12","q13"]:
             if item[0] == "q":
                 qs[int(item[1]), int(item[2])] = load_quiet(int(item[1]), int(item[2]))
             elif item[0] == "w":
-                raws[int(item[1])] = load_raw(w1, int(item[1]), second)
-            elif item[0] == "x":
-                raws[item] = load_raw(w4, int(item[1]), slice(0, N))
-        bf_b1 = {a: cast_w1(raws[a], w1b1_eng[a]) for a in range(K_PASSES) if w1b1_eng[a] != "v"}
-        h0 = []
-        vcast = [3,3,3]
-        for t in range(PACK):
-            h0.append(scores(0, t, qs[0, t]))
-            for a in range(K_PASSES):
-                if vcast[a] == t:
-                    if w1b1_eng[a] == "v":
-                        bf_b1[a] = cast_w1(raws[a], "v")
-                    quant_w1(a, 1, bf_b1[a])
-        a0 = ring.tile([P, PACK, M], F32, name="a0", tag="a0")
-        c0 = ring.tile([P, PACK, M], F32, name="c0", tag="c0")
-        a1 = [keep.tile([P, PACK, HALF], F32, name="a1%d" % u) for u in range(2)]
-        c1 = [keep.tile([P, PACK, HALF], F32, name="c1%d" % u) for u in range(2)]
-        for t in range(PACK):
-            looks(0, t, h0[t], a0, c0, slice(0, M))
-            contrast(t, a0, c0)
-            if how[0][0] == "g":
-                scale(nc.gpsimd, 0, t, a0, c0)
-
-        raw4, bf4 = [raws["x0"], raws["x1"]], {}
-        w4_load, w4_cast = [0,1], [9,0]
-        h1 = []
-        for t in range(PACK):
-            q = qs[1, t]
-            if t in w4_cast:
-                b = w4_cast.index(t)
-                bf4[b] = cast_w4(raw4[b], w4_eng[b], ["h03","bf4"][b])
-            h1.append(scores(1, t, q))
-            for u in range(2):
-                looks(1, t, h1[t], a1[u], c1[u], slice(u * HALF, (u + 1) * HALF))
-                contrast(t, a1[u], c1[u])
-                if how[1 + u][0] == "g":
-                    scale(nc.gpsimd, 1, t, a1[u], c1[u])
+                raws[item] = load_raw(w1, int(item[1]), second, tags[item])
+            else:
+                raws[item] = load_raw(w4, int(item[1]), slice(0, N), tags[item])
         for quad in range(4):
             nc.sync.dma_start(
                 out=w3_sc[32 * quad : 32 * quad + 4, :, :].bitcast(I32),
                 in_=w3_scales[:, 4 * quad : 4 * quad + 4, :].rearrange("b r n -> r b n").bitcast(I32),
             )
         nc.sync.dma_start(out=w3_t[:].bitcast(I32), in_=w3_words.rearrange("b p n -> p b n").bitcast(I32))
-        duty_t = ring.tile([P, N_TILES, M], F32, name="duty_t", tag="raw", bufs=5)
+        duty_t = ring.tile([P, N_TILES, M], F32, name="duty_t", tag=tags["duty"])
         nc.sync.dma_start(out=duty_t[:], in_=duty.rearrange("(n p) m -> p n m", p=P))
 
-
-        d0 = quant_d(0, a0, c0, M, "d0", how[0], "h01")
-        for b in range(R_PASSES):
-            if b not in bf4:
-                bf4[b] = cast_w4(raw4[b], w4_eng[b], ["h03","bf4"][b])
-            quant_w4(b, bf4[b])
-        d1 = [quant_d(1, a1[0], c1[0], HALF, "d10", how[1], "quiet2")]
+        w1b1_eng = ["s","v","v"]
+        vcast = [2,2,2]
+        bf_b1 = {a: cast_w1(raws["w%d" % a], "s", "bf%d" % a) for a in range(K_PASSES) if w1b1_eng[a] == "s"}
+        h0 = []
+        for t in range(PACK):
+            h0.append(scores(0, t, qs[0, t]))
+            for a in range(K_PASSES):
+                if vcast[a] == t and w1b1_eng[a] == "v":
+                    bf_b1[a] = cast_w1(raws["w%d" % a], "v", "bf%d" % a)
+            for a in range(K_PASSES):
+                if vcast[a] == t:
+                    quant_w1(a, 1, bf_b1[a])
+        look_tiles("d0")
+        for t in range(PACK):
+            looks(0, t, h0[t], "d0", slice(0, M))
+            diff_on_gpsimd("d0", t)
+        look_tiles("d10")
+        look_tiles("d11")
+        h1 = []
+        for t in range(PACK):
+            h1.append(scores(1, t, qs[1, t]))
+            looks(1, t, h1[t], "d10", slice(0, HALF))
+            diff_on_gpsimd("d10", t)
+            looks(1, t, h1[t], "d11", slice(HALF, M))
+            diff_on_gpsimd("d11", t)
 
         def readings(u):
             cols = slice(u * HALF, (u + 1) * HALF)
-            rhs = [d0[0][:, cols].bitcast(FP8X4), d1[u][0][:].bitcast(FP8X4)]
-            rhs_sc = [d0[1][:, cols], d1[u][1][:]]
-            for n in range(N_TILES):
-                ns = slice(n * P, (n + 1) * P)
-                acc = psum.tile([P, BANK], F32, name="acc", tag="bank")
-                for b in range(R_PASSES):
-                    nc.tensor.matmul_mx(
-                        out=acc[:, 0:HALF], lhsT=w3_t[:, b, 2 * n * P : 2 * (n + 1) * P].bitcast(FP4X4),
-                        lhsT_scale=w3_sc[:, b, ns], rhs=rhs[b], rhs_scale=rhs_sc[b],
-                        start=(b == 0), stop=(b == R_PASSES - 1),
-                    )
-                for b in range(R_PASSES):
-                    nc.tensor.matmul_mx(
-                        out=acc[:, HALF:BANK], lhsT=w4_codes[b][:, ns].bitcast(FP8X4),
-                        lhsT_scale=w4_sc[b][:, ns], rhs=rhs[b], rhs_scale=rhs_sc[b],
-                        start=(b == 0), stop=(b == R_PASSES - 1),
-                    )
-                alarm = ring.tile([P, HALF], F32, name="alarm", tag="alarm", bufs=4)
-                nc.scalar.activation(out=alarm[:], in_=acc[:, 0:HALF], func=ACT.Tanh)
-                (nc.gpsimd if duty_eng[u][n] == "g" else nc.vector).tensor_tensor(out=alarm[:], in0=alarm[:], in1=duty_t[:, n, cols], op=ALU.mult)
-                res = ring.tile([P, HALF], F32, name="res", tag="res", bufs=5)
-                nc.vector.tensor_tensor(out=res[:], in0=acc[:, HALF:BANK], in1=alarm[:], op=ALU.add)
-                nc.sync.dma_start(out=out[ns, cols], in_=res[:])
+            rhs = [d["d0"][0][:, cols].bitcast(FP8X4), d["d1%d" % u][0][:].bitcast(FP8X4)]
+            rhs_sc = [d["d0"][1][:, cols], d["d1%d" % u][1][:]]
+            for g, (n0, n1) in enumerate([[0,2],[2,4],[4,5]]):
+                wide = (n1 - n0) * HALF
+                first_acc = psum.tile([P, BANK], F32, name="acc", tag="bank")
+                if n1 - n0 == 2:
+                    second_acc = psum.tile([P, BANK], F32, name="acc", tag="bank")
+                    acc_a, acc_t = first_acc[:], second_acc[:]
+                else:
+                    acc_a, acc_t = first_acc[:, 0:HALF], first_acc[:, HALF:BANK]
+                for n in range(n0, n1):
+                    for b in range(R_PASSES):
+                        nc.tensor.matmul_mx(
+                            out=acc_a[:, (n - n0) * HALF : (n - n0 + 1) * HALF],
+                            lhsT=w3_t[:, b, 2 * n * P : 2 * (n + 1) * P].bitcast(FP4X4),
+                            lhsT_scale=w3_sc[:, b, n * P : (n + 1) * P], rhs=rhs[b], rhs_scale=rhs_sc[b],
+                            start=(b == 0), stop=(b == R_PASSES - 1),
+                        )
+                for n in range(n0, n1):
+                    for b in range(R_PASSES):
+                        nc.tensor.matmul_mx(
+                            out=acc_t[:, (n - n0) * HALF : (n - n0 + 1) * HALF],
+                            lhsT=w4_codes[b][:, n * P : (n + 1) * P].bitcast(FP8X4),
+                            lhsT_scale=w4_sc[b][:, n * P : (n + 1) * P], rhs=rhs[b], rhs_scale=rhs_sc[b],
+                            start=(b == 0), stop=(b == R_PASSES - 1),
+                        )
+                alarm = ring.tile([P, wide], F32, name="alarm", tag="alarm", bufs=3)
+                nc.scalar.activation(out=alarm[:], in_=acc_a, func=ACT.Tanh)
+                by_tile = alarm[:].rearrange("p (n m) -> p n m", m=HALF)
+                eng = nc.gpsimd if ["vvv","vvv"][u][g] == "g" else nc.vector
+                eng.tensor_tensor(out=by_tile, in0=by_tile, in1=duty_t[:, n0:n1, cols], op=ALU.mult)
+                res = ring.tile([P, wide], F32, name="res", tag="res", bufs=4)
+                nc.vector.tensor_tensor(out=res[:], in0=acc_t, in1=alarm[:], op=ALU.add)
+                nc.sync.dma_start(
+                    out=out[n0 * P : n1 * P, cols].rearrange("(n p) m -> p n m", p=P),
+                    in_=res[:].rearrange("p (n m) -> p n m", m=HALF),
+                )
 
-
-        readings(0)
-        d1.append(quant_d(1, a1[1], c1[1], HALF, "d11", how[2], "quiet3"))
-        readings(1)
+        d = {}
+        for step in ["c0","c1","f0","d0","q0","f10","d10","f11","q1","d11","r0","r1"]:
+            if step[0] == "d":
+                d[step] = quant_d(int(step[1]), step)
+            elif step[0] == "f":
+                diff_on_vector("d" + step[1:])
+            elif step[0] == "c":
+                cast_w4(int(step[1]))
+            elif step[0] == "q":
+                quant_w4(int(step[1]))
+            elif step[0] == "r":
+                readings(int(step[1]))
+            else:
+                look_tiles("d11")
+                for t in range(PACK):
+                    looks(1, t, h1[t], "d11", slice(HALF, M))
+                    diff_on_gpsimd("d11", t)

@@ -82,10 +82,19 @@ def tile_list_ammonia_leak_watch_kernel(
             else:
                 nc.vector.tensor_copy(out=out, in_=in_)
 
+        one = keep.tile([P, PACK], F32, name="one")
+        nc.vector.memset(one[:], 1.0)
         w1_codes, w1_sc = {}, {}
 
         def cast_w1(raw, eng, tag):
             bf = ring.tile([P, PACK * K_PASS], BF16, name="bf", tag=tag, align_bytes=64)
+            if eng == "g":
+                dst = bf[:].rearrange("p (t m j) -> p t m j", t=PACK, j=PACK)
+                src = raw[:].rearrange("p j (m t) -> p t m j", t=PACK)
+                ones = one[:].unsqueeze(1).to_broadcast([P, P, PACK])
+                for t in range(PACK):
+                    nc.gpsimd.tensor_tensor(out=dst[:, t], in0=src[:, t], in1=ones, op=ALU.mult)
+                return bf
             copy_on(
                 eng,
                 bf[:].rearrange("p (t m j) -> p m j t", t=PACK, j=PACK),
@@ -109,9 +118,10 @@ def tile_list_ammonia_leak_watch_kernel(
                 )
 
         def gather_scales():
+            both = keep.tile([P, S], U8, name="vs", tag="tab0", align_bytes=64)
             for s in range(2):
-                v_sc[s] = keep.tile([P, BANK], U8, name="vs%d" % s, align_bytes=64)
-                nc.vector.tensor_copy(v_sc[s][:], tab_sc[:].indirect(offs_t[:, 32 * s : 32 * (s + 1)]))
+                v_sc[s] = both[:, s * BANK : (s + 1) * BANK]
+                nc.vector.tensor_copy(v_sc[s], tab_sc[:].indirect(offs_t[:, 32 * s : 32 * (s + 1)]))
 
         first = slice(0, K_PASS)
         second = slice(K_PASS, 2 * K_PASS)
@@ -120,17 +130,17 @@ def tile_list_ammonia_leak_watch_kernel(
         raw1 = load_raw(w1, 1, first, "r1")
         raw2 = load_raw(w1, 2, first, "r2")
         load_tab(1)
+        load_tab(2)
+        qs = {(0, 0): load_quiet(0, 0)}
         nc.sync.dma_start(pos1_t[:], pos1)
-        nc.sync.dma_start(pos2_t[:], pos2)
+        thr_t = load_vec(thr, "thr_t")
         sharp_t = load_vec(sharp, "sharp_t")
         share_t = load_vec(share, "share_t")
-        thr_t = load_vec(thr, "thr_t")
-        load_tab(2)
-        side_t = load_vec(side, "side_t")
+        nc.sync.dma_start(pos2_t[:], pos2)
 
-        gather_scales()
         bf0 = cast_w1(raw0, "s", "bf0")
         gather_words(0)
+        gather_scales()
         quant_w1(0, 0, bf0)
         bf1 = cast_w1(raw1, "s", "bf1")
         quant_w1(1, 0, bf1)
@@ -183,7 +193,7 @@ def tile_list_ammonia_leak_watch_kernel(
         how = {"d0":"vv","d10":"vv","d11":"sv"}
         tags = {"w0":"r3","w1":"r0","w2":"r1","x0":"r2","x1":"r3","duty":"r0","gd0":"bf2","sd0":"q13","id0":"h01","vd0":"r1","vd10":"q01","vd11":"q00","sd10":"q10","sd11":"h00","id10":"q02","id11":"q03","bf40":"h02","bf41":"h13","w4c0":"q11","w4c1":"q12"}
         width = {"d0": M, "d10": HALF, "d11": HALF}
-        a_t, c_t, dd_g, dd_v = {}, {}, {}, {}
+        a_t, c_t, dd_g, dd_v, ds_g = {}, {}, {}, {}, {}
 
         def look_tiles(piece):
             a_t[piece] = ring.tile([P, PACK, width[piece]], F32, name="a" + piece, tag=tags.get("a" + piece, "a" + piece), align_bytes=64)
@@ -200,6 +210,14 @@ def tile_list_ammonia_leak_watch_kernel(
                     out=dd_g[piece][:, t, :], in0=a_t[piece][:, t, :], in1=c_t[piece][:, t, :], op=ALU.subtract
                 )
 
+                if how[piece][0] == "G":
+                    if piece not in ds_g:
+                        ds_g[piece] = ring.tile([P, PACK, width[piece]], BF16, name="s" + piece, tag=tags["s" + piece], align_bytes=64)
+                    nc.gpsimd.tensor_scalar(
+                        out=ds_g[piece][:, t, :], in0=dd_g[piece][:, t, :], scalar1=side_t[:, int(piece[1]), t : t + 1],
+                        scalar2=0.0, op0=ALU.mult, op1=ALU.add,
+                    )
+
         def diff_on_vector(piece):
             w = width[piece]
             first_v = (list(diff_eng[piece]) + ["v"]).index("v") if "v" in diff_eng[piece] else -1
@@ -214,8 +232,8 @@ def tile_list_ammonia_leak_watch_kernel(
             w = width[piece]
             first_v = (list(diff_eng[piece]) + ["v"]).index("v") if "v" in diff_eng[piece] else -1
             dd = dd_v.get(piece)
-            ds = ring.tile([P, PACK, w], BF16, name="s" + piece, tag=tags["s" + piece], align_bytes=64)
-            for t in range(PACK):
+            ds = ds_g[piece] if piece in ds_g else ring.tile([P, PACK, w], BF16, name="s" + piece, tag=tags["s" + piece], align_bytes=64)
+            for t in range(0 if piece in ds_g else PACK):
                 diff = dd[:, t - first_v, :] if 0 <= first_v <= t else dd_g[piece][:, t, :]
                 if how[piece][0] == "v":
                     nc.vector.tensor_scalar(
@@ -239,6 +257,14 @@ def tile_list_ammonia_leak_watch_kernel(
 
         def cast_w4(b):
             bf4[b] = ring.tile([P, PACK * N], BF16, name="bf4", tag=tags["bf4%d" % b], align_bytes=64)
+            if w4_eng[b] == "G":
+                for m in range(0, N, P):
+                    nc.gpsimd.tensor_scalar(
+                        out=bf4[b][:].rearrange("p (c j) -> p c j", j=PACK)[:, m : m + P],
+                        in0=raws["x%d" % b][:].rearrange("p j c -> p c j")[:, m : m + P],
+                        scalar1=1.0, scalar2=0.0, op0=ALU.mult, op1=ALU.add,
+                    )
+                return
             copy_on(
                 w4_eng[b],
                 bf4[b][:].rearrange("p (c i j) -> p c j i", i=4, j=PACK),
@@ -254,10 +280,12 @@ def tile_list_ammonia_leak_watch_kernel(
                     in_=bf4[b][:, PACK * cols.start : PACK * cols.stop],
                 )
 
-        qs, raws = {}, {}
-        for item in ["q00","q01","w0","q02","w1","q03","w2","x0","q10","x1","q11","q12","q13"]:
+        raws = {}
+        for item in ["q01","w0","q02","w1","q03","w2","x0","q10","x1","s","q11","q12","q13"]:
             if item[0] == "q":
                 qs[int(item[1]), int(item[2])] = load_quiet(int(item[1]), int(item[2]))
+            elif item[0] == "s":
+                side_t = load_vec(side, "side_t")
             elif item[0] == "w":
                 raws[item] = load_raw(w1, int(item[1]), second, tags[item])
             else:
@@ -271,9 +299,9 @@ def tile_list_ammonia_leak_watch_kernel(
         duty_t = ring.tile([P, N_TILES, M], F32, name="duty_t", tag=tags["duty"])
         nc.sync.dma_start(out=duty_t[:], in_=duty.rearrange("(n p) m -> p n m", p=P))
 
-        w1b1_eng = ["s","v","v"]
-        vcast = [2,2,2]
-        bf_b1 = {a: cast_w1(raws["w%d" % a], "s", "bf%d" % a) for a in range(K_PASSES) if w1b1_eng[a] == "s"}
+        w1b1_eng = ["g","s","v"]
+        vcast = [3,3,3]
+        bf_b1 = {a: cast_w1(raws["w%d" % a], w1b1_eng[a], "bf%d" % a) for a in range(K_PASSES) if w1b1_eng[a] != "v"}
         h0 = []
         for t in range(PACK):
             h0.append(scores(0, t, qs[0, t]))

@@ -19,12 +19,19 @@ AXIS = mybir.AxisListType
 
 P = 128
 PACK = 4
-K_PASS = P * PACK
+PASS = P * PACK
 BANK = 512
-K_PASSES = K // K_PASS
-R_PASSES = H // K_PASS
+K_PASSES = K // PASS
+R_PASSES = H // PASS
 N_TILES = N // P
 HALF = M // 2
+ENTRIES = 16
+QUADS = 4
+SCALE_ROWS = 4
+LINE = 4
+ALIGN = 64
+WIDE_QUANT = 512
+GROUPS = [(n, min(n + 2, N_TILES)) for n in range(0, N_TILES, 2)]
 
 
 def tile_list_ammonia_leak_watch_kernel(
@@ -38,31 +45,32 @@ def tile_list_ammonia_leak_watch_kernel(
         ring = ctx.enter_context(tc.tile_pool(name="ring", bufs=1))
         psum = ctx.enter_context(tc.psum_pool(name="psum", bufs=8))
 
-        offs_t = lists.tile([P, S // 16], U16, name="offs_t")
-        pos1_t = lists.tile([P, M // 16], U16, name="pos1_t")
-        pos2_t = lists.tile([P, M // 16], U16, name="pos2_t")
+        offs_t = lists.tile([P, S // ENTRIES], U16, name="offs_t")
+        pos1_t = lists.tile([P, M // ENTRIES], U16, name="pos1_t")
+        pos2_t = lists.tile([P, M // ENTRIES], U16, name="pos2_t")
 
-        tab_t = [keep.tile([P, T], I32, name="tab%d" % a, align_bytes=64) for a in range(K_PASSES)]
-        tab_sc = keep.tile([P, T], U8, name="tab_sc", tag="vc1", align_bytes=64)
-        w3_sc = keep.tile([P, R_PASSES, N], U8, name="w3_sc", align_bytes=64)
-        w3_t = keep.tile([P, R_PASSES, 2 * N], U8, name="w3_t", align_bytes=64)
+        tab_t = [keep.tile([P, T], I32, name="tab%d" % a, align_bytes=ALIGN) for a in range(K_PASSES)]
+        tab_sc = keep.tile([P, T], U8, name="tab_sc", tag="v_words1", align_bytes=ALIGN)
+        w3_sc = keep.tile([P, R_PASSES, N], U8, name="w3_sc", align_bytes=ALIGN)
+        w3_t = keep.tile([P, R_PASSES, 2 * N], U8, name="w3_t", align_bytes=ALIGN)
 
-        def load_raw(weight, a, cols, tag):
+        def load_weight(weight, g, cols, tag):
             raw = ring.tile([P, PACK, cols.stop - cols.start], F32, name="raw", tag=tag)
-            rows = weight[a * K_PASS : (a + 1) * K_PASS, cols]
+            rows = weight[g * PASS : (g + 1) * PASS, cols]
             nc.sync.dma_start(out=raw[:], in_=rows.rearrange("(p j) c -> p j c", j=PACK))
             return raw
 
-        def load_tab(a):
+        def load_table(a):
             nc.sync.dma_start(out=tab_t[a][:], in_=tab_words[a].rearrange("p t i -> p (t i)").bitcast(I32))
 
-        def load_quiet(b, t):
-            q = ring.tile([P, S], F32, name="q", tag="q%d%d" % (b, t), align_bytes=64)
-            rows = quiet[b * K_PASS : (b + 1) * K_PASS, :].rearrange("(p t) j -> p t j", t=PACK)
-            nc.sync.dma_start(out=q[:], in_=rows[:, t, :])
-            return q
+        quiet_t = {}
 
-        def load_vec(vec, name):
+        def load_quiet(b, t):
+            quiet_t[b, t] = ring.tile([P, S], F32, name="quiet_t", tag="quiet%d%d" % (b, t), align_bytes=ALIGN)
+            rows = quiet[b * PASS : (b + 1) * PASS, :].rearrange("(p t) j -> p t j", t=PACK)
+            nc.sync.dma_start(out=quiet_t[b, t][:], in_=rows[:, t, :])
+
+        def load_rows(vec, name):
             v = keep.tile([P, R_PASSES, PACK], F32, name=name)
             nc.sync.dma_start(out=v[:], in_=vec.rearrange("(b p t) -> p b t", p=P, t=PACK))
             return v
@@ -70,107 +78,95 @@ def tile_list_ammonia_leak_watch_kernel(
         nc.gpsimd.memset(tab_sc[:].bitcast(I32), 0)
         nc.vector.memset(w3_sc[:].bitcast(I32), 0)
         nc.sync.dma_start(offs_t[:], offs)
-        for quad in range(4):
+        for quad in range(QUADS):
             nc.gpsimd.dma_start(
-                out=tab_sc[32 * quad : 32 * quad + 4 * K_PASSES, :].bitcast(I32),
-                in_=tab_scales[:, 4 * quad : 4 * quad + 4, :].bitcast(I32),
+                out=tab_sc[32 * quad : 32 * quad + SCALE_ROWS * K_PASSES, :].bitcast(I32),
+                in_=tab_scales[:, SCALE_ROWS * quad : SCALE_ROWS * (quad + 1), :].bitcast(I32),
             )
-
-        def copy_on(eng, out, in_):
-            if eng == "s":
-                nc.scalar.copy(out=out, in_=in_)
-            else:
-                nc.vector.tensor_copy(out=out, in_=in_)
-
         one = keep.tile([P, PACK], F32, name="one")
         nc.vector.memset(one[:], 1.0)
-        w1_codes, w1_sc = {}, {}
 
-        def cast_w1(raw, eng, tag):
-            bf = ring.tile([P, PACK * K_PASS], BF16, name="bf", tag=tag, align_bytes=64)
-            if eng == "g":
-                dst = bf[:].rearrange("p (t m j) -> p t m j", t=PACK, j=PACK)
-                src = raw[:].rearrange("p j (m t) -> p t m j", t=PACK)
-                ones = one[:].unsqueeze(1).to_broadcast([P, P, PACK])
-                for t in range(PACK):
-                    nc.gpsimd.tensor_tensor(out=dst[:, t], in0=src[:, t], in1=ones, op=ALU.mult)
-                return bf
-            copy_on(
-                eng,
-                bf[:].rearrange("p (t m j) -> p m j t", t=PACK, j=PACK),
-                raw[:].rearrange("p j (m t) -> p m j t", t=PACK),
+        def round_w1(copy, raw, a):
+            bf = ring.tile([P, PACK * PASS], BF16, name="w1_bf", tag="bf%d" % a, align_bytes=ALIGN)
+            copy(
+                out=bf[:].rearrange("p (t m j) -> p m j t", t=PACK, j=PACK),
+                in_=raw[:].rearrange("p j (m t) -> p m j t", t=PACK),
             )
             return bf
 
-        def quant_w1(a, b, bf):
-            w1_codes[a, b] = ring.tile([P, K_PASS], U32, name="w1c%d%d" % (a, b), tag={}.get("%d%d" % (a, b), "w1c%d%d" % (a, b)), align_bytes=64)
-            w1_sc[a, b] = keep.tile([P, K_PASS], U8, name="w1s%d%d" % (a, b), align_bytes=64)
+        def round_w1_on_gpsimd(raw, a):
+            bf = ring.tile([P, PACK * PASS], BF16, name="w1_bf", tag="bf%d" % a, align_bytes=ALIGN)
+            dst = bf[:].rearrange("p (t m j) -> p t m j", t=PACK, j=PACK)
+            src = raw[:].rearrange("p j (m t) -> p t m j", t=PACK)
+            ones = one[:].unsqueeze(1).to_broadcast([P, P, PACK])
+            for t in range(PACK):
+                nc.gpsimd.tensor_tensor(out=dst[:, t], in0=src[:, t], in1=ones, op=ALU.mult)
+            return bf
+
+        w1_codes, w1_sc = {}, {}
+
+        def quantise_w1(a, b, bf):
+            w1_codes[a, b] = ring.tile([P, PASS], U32, name="w1_codes%d%d" % (a, b), align_bytes=ALIGN)
+            w1_sc[a, b] = keep.tile([P, PASS], U8, name="w1_sc%d%d" % (a, b), align_bytes=ALIGN)
             nc.vector.quantize_mx(out=w1_codes[a, b][:].bitcast(FP8X4), scales=w1_sc[a, b][:], in_=bf[:])
 
-        v_codes, v_sc = {}, {}
+        v_words = {}
 
-        def gather_words(a):
-            v_codes[a] = keep.tile([P, S], U32, name="vc%d" % a, align_bytes=64)
-            for s in range(2):
+        def gather_words(a, step):
+            v_words[a] = keep.tile([P, S], U32, name="v_words%d" % a, align_bytes=ALIGN)
+            for c in range(0, S, step):
                 nc.vector.tensor_copy(
-                    v_codes[a][:, s * BANK : (s + 1) * BANK],
-                    tab_t[a][:].bitcast(U32).indirect(offs_t[:, 32 * s : 32 * (s + 1)]),
+                    v_words[a][:, c : c + step],
+                    tab_t[a][:].bitcast(U32).indirect(offs_t[:, c // ENTRIES : (c + step) // ENTRIES]),
                 )
 
-        def gather_scales():
-            both = keep.tile([P, S], U8, name="vs", tag="tab0", align_bytes=64)
-            for s in range(2):
-                v_sc[s] = both[:, s * BANK : (s + 1) * BANK]
-                nc.vector.tensor_copy(v_sc[s], tab_sc[:].indirect(offs_t[:, 32 * s : 32 * (s + 1)]))
-
-        first = slice(0, K_PASS)
-        second = slice(K_PASS, 2 * K_PASS)
-        raw0 = load_raw(w1, 0, first, "r0")
-        load_tab(0)
-        raw1 = load_raw(w1, 1, first, "r1")
-        raw2 = load_raw(w1, 2, first, "r2")
-        load_tab(1)
-        load_tab(2)
-        qs = {(0, 0): load_quiet(0, 0)}
+        halves = [slice(b * PASS, (b + 1) * PASS) for b in range(R_PASSES)]
+        raw0 = load_weight(w1, 0, halves[0], "raw0")
+        load_table(0)
+        raw1 = load_weight(w1, 1, halves[0], "raw1")
+        raw2 = load_weight(w1, 2, halves[0], "raw2")
+        load_table(1)
+        load_table(2)
+        load_quiet(0, 0)
         nc.sync.dma_start(pos1_t[:], pos1)
-        thr_t = load_vec(thr, "thr_t")
-        sharp_t = load_vec(sharp, "sharp_t")
-        share_t = load_vec(share, "share_t")
+        thr_t = load_rows(thr, "thr_t")
+        sharp_t = load_rows(sharp, "sharp_t")
+        share_t = load_rows(share, "share_t")
         nc.sync.dma_start(pos2_t[:], pos2)
 
-        bf0 = cast_w1(raw0, "s", "bf0")
-        gather_words(0)
-        gather_scales()
-        quant_w1(0, 0, bf0)
-        bf1 = cast_w1(raw1, "s", "bf1")
-        quant_w1(1, 0, bf1)
-        bf2 = cast_w1(raw2, "s", "bf2")
-        gather_words(1)
-        quant_w1(2, 0, bf2)
-        gather_words(2)
+        bf0 = round_w1(nc.scalar.copy, raw0, 0)
+        gather_words(0, S)
+        v_sc = keep.tile([P, S], U8, name="v_sc", tag="tab0", align_bytes=ALIGN)
+        nc.vector.tensor_copy(v_sc[:], tab_sc[:].indirect(offs_t[:]))
+        quantise_w1(0, 0, bf0)
+        bf1 = round_w1(nc.scalar.copy, raw1, 1)
+        quantise_w1(1, 0, bf1)
+        bf2 = round_w1(nc.scalar.copy, raw2, 2)
+        gather_words(1, S)
+        quantise_w1(2, 0, bf2)
+        gather_words(2, BANK)
 
-        slope = keep.tile([P, R_PASSES, PACK], F32, name="slope")
+        slope = ring.tile([P, R_PASSES, PACK], F32, name="slope", align_bytes=ALIGN)
         nc.gpsimd.tensor_tensor(out=slope[:], in0=sharp_t[:], in1=share_t[:], op=ALU.mult)
-        top = keep.tile([P, R_PASSES, PACK], F32, name="top")
+        top = ring.tile([P, R_PASSES, PACK], F32, name="top", align_bytes=ALIGN)
         c_bias = keep.tile([P, R_PASSES, PACK], F32, name="c_bias")
 
-        def scores(b, t, q):
-            h = ring.tile([P, S], F32, name="h", tag="h%d%d" % (b, t), align_bytes=64)
-            order = [0,1,2] if b else [0, 1, 2]
-            for s in range(2):
+        def scores(b, t):
+            h = ring.tile([P, S], F32, name="h", tag="h%d%d" % (b, t), align_bytes=ALIGN)
+            for s in range(S // BANK):
                 cols = slice(s * BANK, (s + 1) * BANK)
                 acc = psum.tile([P, BANK], F32, name="acc", tag="bank")
-                for a in order:
+                for a in range(K_PASSES):
                     nc.tensor.matmul_mx(
                         out=acc[:],
                         lhsT=w1_codes[a, b][:, t * P : (t + 1) * P].bitcast(FP8X4),
                         lhsT_scale=w1_sc[a, b][:, t * P : (t + 1) * P],
-                        rhs=v_codes[a][:, cols].bitcast(FP8X4),
-                        rhs_scale=v_sc[s][4 * a : P, :],
-                        start=(a == order[0]),
-                        stop=(a == order[-1]),
+                        rhs=v_words[a][:, cols].bitcast(FP8X4),
+                        rhs_scale=v_sc[SCALE_ROWS * a : P, cols],
+                        start=(a == 0),
+                        stop=(a == K_PASSES - 1),
                     )
-                nc.vector.tensor_tensor(out=h[:, cols], in0=acc[:], in1=q[:, cols], op=ALU.max)
+                nc.vector.tensor_tensor(out=h[:, cols], in0=acc[:], in1=quiet_t[b, t][:, cols], op=ALU.max)
             nc.vector.tensor_reduce(out=top[:, b, t : t + 1], in_=h[:], axis=AXIS.X, op=ALU.max)
             nc.vector.tensor_scalar(
                 out=c_bias[:, b, t : t + 1], in0=top[:, b, t : t + 1], scalar1=slope[:, b, t : t + 1],
@@ -178,207 +174,169 @@ def tile_list_ammonia_leak_watch_kernel(
             )
             return h
 
-        def looks(b, t, h, piece, cols):
-            entries = slice(cols.start // 16, cols.stop // 16)
+        def looks(b, t, h, a_t, c_t, cols):
+            entries = slice(cols.start // ENTRIES, cols.stop // ENTRIES)
             nc.scalar.activation(
-                out=a_t[piece][:, t, :], in_=h[:].indirect(pos1_t[:, entries]), func=ACT.Sigmoid,
+                out=a_t[:, t, :], in_=h[:].indirect(pos1_t[:, entries]), func=ACT.Sigmoid,
                 bias=thr_t[:, b, t : t + 1],
             )
             nc.scalar.activation(
-                out=c_t[piece][:, t, :], in_=h[:].indirect(pos2_t[:, entries]), func=ACT.Sigmoid,
+                out=c_t[:, t, :], in_=h[:].indirect(pos2_t[:, entries]), func=ACT.Sigmoid,
                 bias=c_bias[:, b, t : t + 1], scale=sharp_t[:, b, t : t + 1],
             )
 
-        diff_eng = {"d0":"gggg","d10":"vvvv","d11":"vvvv"}
-        how = {"d0":"vv","d10":"vv","d11":"sv"}
-        tags = {"w0":"r3","w1":"r0","w2":"r1","x0":"r2","x1":"r3","duty":"r0","gd0":"bf2","sd0":"q13","id0":"h01","vd0":"r1","vd10":"q01","vd11":"q00","sd10":"q10","sd11":"h00","id10":"q02","id11":"q03","bf40":"h02","bf41":"h13","w4c0":"q11","w4c1":"q12"}
-        width = {"d0": M, "d10": HALF, "d11": HALF}
-        a_t, c_t, dd_g, dd_v, ds_g = {}, {}, {}, {}, {}
-
-        def look_tiles(piece):
-            a_t[piece] = ring.tile([P, PACK, width[piece]], F32, name="a" + piece, tag=tags.get("a" + piece, "a" + piece), align_bytes=64)
-            c_t[piece] = ring.tile([P, PACK, width[piece]], F32, name="c" + piece, tag=tags.get("c" + piece, "c" + piece), align_bytes=64)
-
-        def diff_on_gpsimd(piece, t):
-            if diff_eng[piece][t] == "g":
-                if piece not in dd_g:
-                    if "g" + piece in tags:
-                        dd_g[piece] = ring.tile([P, PACK, width[piece]], F32, name="g" + piece, tag=tags["g" + piece], align_bytes=64)
-                    else:
-                        dd_g[piece] = a_t[piece]
-                nc.gpsimd.tensor_tensor(
-                    out=dd_g[piece][:, t, :], in0=a_t[piece][:, t, :], in1=c_t[piece][:, t, :], op=ALU.subtract
-                )
-
-                if how[piece][0] == "G":
-                    if piece not in ds_g:
-                        ds_g[piece] = ring.tile([P, PACK, width[piece]], BF16, name="s" + piece, tag=tags["s" + piece], align_bytes=64)
-                    nc.gpsimd.tensor_scalar(
-                        out=ds_g[piece][:, t, :], in0=dd_g[piece][:, t, :], scalar1=side_t[:, int(piece[1]), t : t + 1],
-                        scalar2=0.0, op0=ALU.mult, op1=ALU.add,
-                    )
-
-        def diff_on_vector(piece):
-            w = width[piece]
-            first_v = (list(diff_eng[piece]) + ["v"]).index("v") if "v" in diff_eng[piece] else -1
-            if first_v >= 0:
-                dd = ring.tile([P, PACK - first_v, w], F32, name="v" + piece, tag=tags["v" + piece], align_bytes=64)
-                nc.vector.tensor_tensor(
-                    out=dd[:], in0=a_t[piece][:, first_v:PACK, :], in1=c_t[piece][:, first_v:PACK, :], op=ALU.subtract
-                )
-                dd_v[piece] = dd
-
-        def quant_d(b, piece):
-            w = width[piece]
-            first_v = (list(diff_eng[piece]) + ["v"]).index("v") if "v" in diff_eng[piece] else -1
-            dd = dd_v.get(piece)
-            ds = ds_g[piece] if piece in ds_g else ring.tile([P, PACK, w], BF16, name="s" + piece, tag=tags["s" + piece], align_bytes=64)
-            for t in range(0 if piece in ds_g else PACK):
-                diff = dd[:, t - first_v, :] if 0 <= first_v <= t else dd_g[piece][:, t, :]
-                if how[piece][0] == "v":
-                    nc.vector.tensor_scalar(
-                        out=ds[:, t, :], in0=diff, scalar1=side_t[:, b, t : t + 1], scalar2=None, op0=ALU.mult
-                    )
-                else:
-                    nc.scalar.activation(out=ds[:, t, :], in_=diff, func=ACT.Copy, scale=side_t[:, b, t : t + 1])
-            bf = ring.tile([P, w * PACK], BF16, name="i" + piece, tag=tags["i" + piece], align_bytes=64)
-            copy_on(
-                how[piece][1],
-                bf[:].rearrange("p (c i t) -> p c t i", i=4, t=PACK),
-                ds[:].rearrange("p t (c i) -> p c t i", i=4),
+        w1_raw = [load_weight(w1, 0, halves[1], "raw3")]
+        load_quiet(0, 1)
+        side_t = load_rows(side, "side_t")
+        w1_raw.append(load_weight(w1, 1, halves[1], "raw0"))
+        load_quiet(0, 2)
+        load_quiet(0, 3)
+        w1_raw.append(load_weight(w1, 2, halves[1], "raw1"))
+        w4_raw = [load_weight(w4, 0, slice(0, N), "raw2")]
+        load_quiet(1, 0)
+        w4_raw.append(load_weight(w4, 1, slice(0, N), "raw3"))
+        for t in range(1, PACK):
+            load_quiet(1, t)
+        for quad in range(QUADS):
+            rows = w3_scales[:, SCALE_ROWS * quad : SCALE_ROWS * (quad + 1), :]
+            nc.sync.dma_start(
+                out=w3_sc[32 * quad : 32 * quad + SCALE_ROWS, :, :].bitcast(I32),
+                in_=rows.rearrange("b r n -> r b n").bitcast(I32),
             )
-            codes = ring.tile([P, w], U32, name="q" + piece, tag=tags.get("q" + piece, "q" + piece), align_bytes=64)
-            sc = keep.tile([P, w], U8, name=piece + "s", align_bytes=64)
+        nc.sync.dma_start(out=w3_t[:].bitcast(I32), in_=w3_words.rearrange("b p n -> p b n").bitcast(I32))
+        duty_t = ring.tile([P, N_TILES, M], F32, name="duty_t", tag="raw0")
+        nc.sync.dma_start(out=duty_t[:], in_=duty.rearrange("(n p) m -> p n m", p=P))
+
+        w1_bf = [round_w1_on_gpsimd(w1_raw[0], 0), round_w1(nc.scalar.copy, w1_raw[1], 1)]
+        h0 = [scores(0, t) for t in range(PACK - 1)]
+        w1_bf.append(round_w1(nc.vector.tensor_copy, w1_raw[2], 2))
+        for a in range(K_PASSES):
+            quantise_w1(a, 1, w1_bf[a])
+        h0.append(scores(0, PACK - 1))
+
+        a0 = ring.tile([P, PACK, M], F32, name="a0", align_bytes=ALIGN)
+        c0 = ring.tile([P, PACK, M], F32, name="c0", align_bytes=ALIGN)
+        diff0 = ring.tile([P, PACK, M], F32, name="diff0", tag="bf2", align_bytes=ALIGN)
+        for t in range(PACK):
+            looks(0, t, h0[t], a0, c0, slice(0, M))
+            nc.gpsimd.tensor_tensor(out=diff0[:, t, :], in0=a0[:, t, :], in1=c0[:, t, :], op=ALU.subtract)
+
+        a1, c1 = [], []
+        for u in range(2):
+            a1.append(ring.tile([P, PACK, HALF], F32, name="a1%d" % u, align_bytes=ALIGN))
+            c1.append(ring.tile([P, PACK, HALF], F32, name="c1%d" % u, align_bytes=ALIGN))
+        for t in range(PACK):
+            h = scores(1, t)
+            for u in range(2):
+                looks(1, t, h, a1[u], c1[u], slice(u * HALF, (u + 1) * HALF))
+
+        def interleave(copy, src, dst):
+            copy(
+                out=dst[:].rearrange("p (c i j) -> p c j i", i=LINE, j=PACK),
+                in_=src[:].rearrange("p j (c i) -> p c j i", i=LINE),
+            )
+
+        w4_bf = [
+            ring.tile([P, PACK * N], BF16, name="w4_bf0", tag="slope", align_bytes=ALIGN),
+            ring.tile([P, PACK * N], BF16, name="w4_bf1", tag="h13", align_bytes=ALIGN),
+        ]
+        interleave(nc.vector.tensor_copy, w4_raw[0], w4_bf[0])
+        interleave(nc.scalar.copy, w4_raw[1], w4_bf[1])
+        w4_codes, w4_sc = {}, {}
+
+        def quantise_w4(b, tag):
+            w4_codes[b] = ring.tile([P, N], U32, name="w4_codes", tag=tag, align_bytes=ALIGN)
+            w4_sc[b] = keep.tile([P, N], U8, name="w4_sc%d" % b, align_bytes=ALIGN)
+            for cols in (slice(0, WIDE_QUANT), slice(WIDE_QUANT, N)):
+                nc.vector.quantize_mx(
+                    out=w4_codes[b][:, cols].bitcast(FP8X4), scales=w4_sc[b][:, cols],
+                    in_=w4_bf[b][:, PACK * cols.start : PACK * cols.stop],
+                )
+
+        def quantise_d(bf, width, name, tag):
+            codes = ring.tile([P, width], U32, name="d_codes", tag=tag, align_bytes=ALIGN)
+            sc = keep.tile([P, width], U8, name=name, align_bytes=ALIGN)
             nc.vector.quantize_mx(out=codes[:].bitcast(FP8X4), scales=sc[:], in_=bf[:])
             return codes, sc
 
-        w4_codes, w4_sc, bf4 = {}, {}, {}
-        w4_eng = ["s","s"]
+        def difference(u, tag):
+            diff = ring.tile([P, PACK, HALF], F32, name="diff1", tag=tag, align_bytes=ALIGN)
+            nc.vector.tensor_tensor(out=diff[:], in0=a1[u][:], in1=c1[u][:], op=ALU.subtract)
+            return diff
 
-        def cast_w4(b):
-            bf4[b] = ring.tile([P, PACK * N], BF16, name="bf4", tag=tags["bf4%d" % b], align_bytes=64)
-            if w4_eng[b] == "G":
-                for m in range(0, N, P):
-                    nc.gpsimd.tensor_scalar(
-                        out=bf4[b][:].rearrange("p (c j) -> p c j", j=PACK)[:, m : m + P],
-                        in0=raws["x%d" % b][:].rearrange("p j c -> p c j")[:, m : m + P],
-                        scalar1=1.0, scalar2=0.0, op0=ALU.mult, op1=ALU.add,
+        quantise_w4(0, "quiet11")
+
+        d0_bf = ring.tile([P, M * PACK], BF16, name="d0_bf", tag="h01", align_bytes=ALIGN)
+        for c in range(0, M, P):
+            nc.gpsimd.tensor_tensor(
+                out=d0_bf[:].rearrange("p (m t) -> p m t", t=PACK)[:, c : c + P],
+                in0=diff0[:].rearrange("p t m -> p m t")[:, c : c + P],
+                in1=side_t[:, 0, :].unsqueeze(1).to_broadcast([P, P, PACK]),
+                op=ALU.mult,
+            )
+        d0 = quantise_d(d0_bf, M, "d0_sc", "top")
+
+        diff = difference(0, "quiet01")
+        rounded = ring.tile([P, PACK, HALF], BF16, name="rounded", tag="quiet10", align_bytes=ALIGN)
+        for t in range(PACK):
+            nc.vector.tensor_scalar(
+                out=rounded[:, t, :], in0=diff[:, t, :], scalar1=side_t[:, 1, t : t + 1], scalar2=None,
+                op0=ALU.mult,
+            )
+        d1_bf = ring.tile([P, HALF * PACK], BF16, name="d1_bf", tag="quiet02", align_bytes=ALIGN)
+        interleave(nc.vector.tensor_copy, rounded, d1_bf)
+        d1 = [quantise_d(d1_bf, HALF, "d10_sc", "d10_codes")]
+
+        diff = difference(1, "quiet00")
+        quantise_w4(1, "quiet12")
+        rounded = ring.tile([P, PACK, HALF], BF16, name="rounded", tag="h00", align_bytes=ALIGN)
+        for t in range(PACK):
+            nc.scalar.activation(
+                out=rounded[:, t, :], in_=diff[:, t, :], func=ACT.Copy, scale=side_t[:, 1, t : t + 1]
+            )
+        d1_bf = ring.tile([P, HALF * PACK], BF16, name="d1_bf", tag="quiet03", align_bytes=ALIGN)
+        interleave(nc.scalar.copy, rounded, d1_bf)
+        d1.append(quantise_d(d1_bf, HALF, "d11_sc", "d11_codes"))
+
+        def reading(acc, n0, n1, codes, sc, rhs, rhs_sc):
+            for n in range(n0, n1):
+                for b in range(R_PASSES):
+                    nc.tensor.matmul_mx(
+                        out=acc[:, (n - n0) * HALF : (n - n0 + 1) * HALF],
+                        lhsT=codes(b, n), lhsT_scale=sc(b, n), rhs=rhs[b], rhs_scale=rhs_sc[b],
+                        start=(b == 0), stop=(b == R_PASSES - 1),
                     )
-                return
-            copy_on(
-                w4_eng[b],
-                bf4[b][:].rearrange("p (c i j) -> p c j i", i=4, j=PACK),
-                raws["x%d" % b][:].rearrange("p j (c i) -> p c j i", i=4),
-            )
 
-        def quant_w4(b):
-            w4_codes[b] = ring.tile([P, N], U32, name="w4c%d" % b, tag=tags["w4c%d" % b], align_bytes=64)
-            w4_sc[b] = keep.tile([P, N], U8, name="w4s%d" % b, align_bytes=64)
-            for cols in (slice(0, 512), slice(512, N)):
-                nc.vector.quantize_mx(
-                    out=w4_codes[b][:, cols].bitcast(FP8X4), scales=w4_sc[b][:, cols],
-                    in_=bf4[b][:, PACK * cols.start : PACK * cols.stop],
-                )
-
-        raws = {}
-        for item in ["q01","w0","q02","w1","q03","w2","x0","q10","x1","s","q11","q12","q13"]:
-            if item[0] == "q":
-                qs[int(item[1]), int(item[2])] = load_quiet(int(item[1]), int(item[2]))
-            elif item[0] == "s":
-                side_t = load_vec(side, "side_t")
-            elif item[0] == "w":
-                raws[item] = load_raw(w1, int(item[1]), second, tags[item])
-            else:
-                raws[item] = load_raw(w4, int(item[1]), slice(0, N), tags[item])
-        for quad in range(4):
-            nc.sync.dma_start(
-                out=w3_sc[32 * quad : 32 * quad + 4, :, :].bitcast(I32),
-                in_=w3_scales[:, 4 * quad : 4 * quad + 4, :].rearrange("b r n -> r b n").bitcast(I32),
-            )
-        nc.sync.dma_start(out=w3_t[:].bitcast(I32), in_=w3_words.rearrange("b p n -> p b n").bitcast(I32))
-        duty_t = ring.tile([P, N_TILES, M], F32, name="duty_t", tag=tags["duty"])
-        nc.sync.dma_start(out=duty_t[:], in_=duty.rearrange("(n p) m -> p n m", p=P))
-
-        w1b1_eng = ["g","s","v"]
-        vcast = [3,3,3]
-        bf_b1 = {a: cast_w1(raws["w%d" % a], w1b1_eng[a], "bf%d" % a) for a in range(K_PASSES) if w1b1_eng[a] != "v"}
-        h0 = []
-        for t in range(PACK):
-            h0.append(scores(0, t, qs[0, t]))
-            for a in range(K_PASSES):
-                if vcast[a] == t and w1b1_eng[a] == "v":
-                    bf_b1[a] = cast_w1(raws["w%d" % a], "v", "bf%d" % a)
-            for a in range(K_PASSES):
-                if vcast[a] == t:
-                    quant_w1(a, 1, bf_b1[a])
-        look_tiles("d0")
-        for t in range(PACK):
-            looks(0, t, h0[t], "d0", slice(0, M))
-            diff_on_gpsimd("d0", t)
-        look_tiles("d10")
-        look_tiles("d11")
-        h1 = []
-        for t in range(PACK):
-            h1.append(scores(1, t, qs[1, t]))
-            looks(1, t, h1[t], "d10", slice(0, HALF))
-            diff_on_gpsimd("d10", t)
-            looks(1, t, h1[t], "d11", slice(HALF, M))
-            diff_on_gpsimd("d11", t)
-
-        def readings(u):
+        for u in range(2):
             cols = slice(u * HALF, (u + 1) * HALF)
-            rhs = [d["d0"][0][:, cols].bitcast(FP8X4), d["d1%d" % u][0][:].bitcast(FP8X4)]
-            rhs_sc = [d["d0"][1][:, cols], d["d1%d" % u][1][:]]
-            for g, (n0, n1) in enumerate([[0,2],[2,4],[4,5]]):
-                wide = (n1 - n0) * HALF
-                first_acc = psum.tile([P, BANK], F32, name="acc", tag="bank")
-                if n1 - n0 == 2:
-                    second_acc = psum.tile([P, BANK], F32, name="acc", tag="bank")
-                    acc_a, acc_t = first_acc[:], second_acc[:]
+            rhs = [d0[0][:, cols].bitcast(FP8X4), d1[u][0][:].bitcast(FP8X4)]
+            rhs_sc = [d0[1][:, cols], d1[u][1][:]]
+            for n0, n1 in GROUPS:
+                pair = n1 - n0 == 2
+                bank = psum.tile([P, BANK], F32, name="acc", tag="bank")
+                if pair:
+                    second_bank = psum.tile([P, BANK], F32, name="acc", tag="bank")
+                    acc_alarm, acc_trend = bank[:], second_bank[:]
                 else:
-                    acc_a, acc_t = first_acc[:, 0:HALF], first_acc[:, HALF:BANK]
-                for n in range(n0, n1):
-                    for b in range(R_PASSES):
-                        nc.tensor.matmul_mx(
-                            out=acc_a[:, (n - n0) * HALF : (n - n0 + 1) * HALF],
-                            lhsT=w3_t[:, b, 2 * n * P : 2 * (n + 1) * P].bitcast(FP4X4),
-                            lhsT_scale=w3_sc[:, b, n * P : (n + 1) * P], rhs=rhs[b], rhs_scale=rhs_sc[b],
-                            start=(b == 0), stop=(b == R_PASSES - 1),
-                        )
-                for n in range(n0, n1):
-                    for b in range(R_PASSES):
-                        nc.tensor.matmul_mx(
-                            out=acc_t[:, (n - n0) * HALF : (n - n0 + 1) * HALF],
-                            lhsT=w4_codes[b][:, n * P : (n + 1) * P].bitcast(FP8X4),
-                            lhsT_scale=w4_sc[b][:, n * P : (n + 1) * P], rhs=rhs[b], rhs_scale=rhs_sc[b],
-                            start=(b == 0), stop=(b == R_PASSES - 1),
-                        )
-                alarm = ring.tile([P, wide], F32, name="alarm", tag="alarm", bufs=3)
-                nc.scalar.activation(out=alarm[:], in_=acc_a, func=ACT.Tanh)
+                    acc_alarm, acc_trend = bank[:, 0:HALF], bank[:, HALF:BANK]
+                reading(
+                    acc_alarm, n0, n1,
+                    lambda b, n: w3_t[:, b, 2 * n * P : 2 * (n + 1) * P].bitcast(FP4X4),
+                    lambda b, n: w3_sc[:, b, n * P : (n + 1) * P], rhs, rhs_sc,
+                )
+                reading(
+                    acc_trend, n0, n1,
+                    lambda b, n: w4_codes[b][:, n * P : (n + 1) * P].bitcast(FP8X4),
+                    lambda b, n: w4_sc[b][:, n * P : (n + 1) * P], rhs, rhs_sc,
+                )
+                alarm = ring.tile([P, (n1 - n0) * HALF], F32, name="alarm", bufs=3)
+                nc.scalar.activation(out=alarm[:], in_=acc_alarm, func=ACT.Tanh)
                 by_tile = alarm[:].rearrange("p (n m) -> p n m", m=HALF)
-                eng = nc.gpsimd if ["vvv","vvv"][u][g] == "g" else nc.vector
-                eng.tensor_tensor(out=by_tile, in0=by_tile, in1=duty_t[:, n0:n1, cols], op=ALU.mult)
-                res = ring.tile([P, wide], F32, name="res", tag="res", bufs=4)
-                nc.vector.tensor_tensor(out=res[:], in0=acc_t, in1=alarm[:], op=ALU.add)
+                engine = nc.vector if pair else nc.gpsimd
+                engine.tensor_tensor(out=by_tile, in0=by_tile, in1=duty_t[:, n0:n1, cols], op=ALU.mult)
+                result = ring.tile([P, (n1 - n0) * HALF], F32, name="result", bufs=4)
+                nc.vector.tensor_tensor(out=result[:], in0=acc_trend, in1=alarm[:], op=ALU.add)
                 nc.sync.dma_start(
                     out=out[n0 * P : n1 * P, cols].rearrange("(n p) m -> p n m", p=P),
-                    in_=res[:].rearrange("p (n m) -> p n m", m=HALF),
+                    in_=result[:].rearrange("p (n m) -> p n m", m=HALF),
                 )
-
-        d = {}
-        for step in ["c0","c1","f0","d0","q0","f10","d10","f11","q1","d11","r0","r1"]:
-            if step[0] == "d":
-                d[step] = quant_d(int(step[1]), step)
-            elif step[0] == "f":
-                diff_on_vector("d" + step[1:])
-            elif step[0] == "c":
-                cast_w4(int(step[1]))
-            elif step[0] == "q":
-                quant_w4(int(step[1]))
-            elif step[0] == "r":
-                readings(int(step[1]))
-            else:
-                look_tiles("d11")
-                for t in range(PACK):
-                    looks(1, t, h1[t], "d11", slice(HALF, M))
-                    diff_on_gpsimd("d11", t)

from contextlib import ExitStack

import concourse.mybir as mybir

K, H, N, T, S, M = 1536, 1024, 640, 2048, 1024, 512
FLOPS = 2 * K * H * S + 2 * 2 * H * N * M

F32 = mybir.dt.float32
BF16 = mybir.dt.bfloat16
I32 = mybir.dt.int32
U32 = mybir.dt.uint32
U16 = mybir.dt.uint16
U8 = mybir.dt.uint8
FP8X4 = mybir.dt.float8_e4m3fn_x4
FP4X4 = mybir.dt.float4_e2m1fn_x4
ALU = mybir.AluOpType
ACT = mybir.ActivationFunctionType
AXIS = mybir.AxisListType

P = 128
PACK = 4
PASS = P * PACK
BANK = 512
K_PASSES = K // PASS
R_PASSES = H // PASS
N_TILES = N // P
HALF = M // 2
ENTRIES = 16
QUADS = 4
SCALE_ROWS = 4
LINE = 4
ALIGN = 64
WIDE_QUANT = 512
GROUPS = [(n, min(n + 2, N_TILES)) for n in range(0, N_TILES, 2)]


def tile_list_ammonia_leak_watch_kernel(
    tc, tab_words, tab_scales, offs, pos1, pos2, w1, quiet, thr, sharp, share, side,
    w3_words, w3_scales, w4, duty, out,
):
    nc = tc.nc
    with ExitStack() as ctx:
        lists = ctx.enter_context(tc.tile_pool(name="lists", bufs=1))
        keep = ctx.enter_context(tc.tile_pool(name="keep", bufs=1))
        ring = ctx.enter_context(tc.tile_pool(name="ring", bufs=1))
        psum = ctx.enter_context(tc.psum_pool(name="psum", bufs=8))

        offs_t = lists.tile([P, S // ENTRIES], U16, name="offs_t")
        pos1_t = lists.tile([P, M // ENTRIES], U16, name="pos1_t")
        pos2_t = lists.tile([P, M // ENTRIES], U16, name="pos2_t")

        tab_t = [keep.tile([P, T], I32, name="tab%d" % a, align_bytes=ALIGN) for a in range(K_PASSES)]
        tab_sc = keep.tile([P, T], U8, name="tab_sc", tag="v_words1", align_bytes=ALIGN)
        w3_sc = keep.tile([P, R_PASSES, N], U8, name="w3_sc", align_bytes=ALIGN)
        w3_t = keep.tile([P, R_PASSES, 2 * N], U8, name="w3_t", align_bytes=ALIGN)

        def load_weight(weight, g, cols, tag):
            raw = ring.tile([P, PACK, cols.stop - cols.start], F32, name="raw", tag=tag)
            rows = weight[g * PASS : (g + 1) * PASS, cols]
            nc.sync.dma_start(out=raw[:], in_=rows.rearrange("(p j) c -> p j c", j=PACK))
            return raw

        def load_table(a):
            nc.sync.dma_start(out=tab_t[a][:], in_=tab_words[a].rearrange("p t i -> p (t i)").bitcast(I32))

        quiet_t = {}

        def load_quiet(b, t):
            quiet_t[b, t] = ring.tile([P, S], F32, name="quiet_t", tag="quiet%d%d" % (b, t), align_bytes=ALIGN)
            rows = quiet[b * PASS : (b + 1) * PASS, :].rearrange("(p t) j -> p t j", t=PACK)
            nc.sync.dma_start(out=quiet_t[b, t][:], in_=rows[:, t, :])

        def load_rows(vec, name):
            v = keep.tile([P, R_PASSES, PACK], F32, name=name)
            nc.sync.dma_start(out=v[:], in_=vec.rearrange("(b p t) -> p b t", p=P, t=PACK))
            return v

        nc.gpsimd.memset(tab_sc[:].bitcast(I32), 0)
        nc.vector.memset(w3_sc[:].bitcast(I32), 0)
        nc.sync.dma_start(offs_t[:], offs)
        for quad in range(QUADS):
            nc.gpsimd.dma_start(
                out=tab_sc[32 * quad : 32 * quad + SCALE_ROWS * K_PASSES, :].bitcast(I32),
                in_=tab_scales[:, SCALE_ROWS * quad : SCALE_ROWS * (quad + 1), :].bitcast(I32),
            )
        one = keep.tile([P, PACK], F32, name="one")
        nc.vector.memset(one[:], 1.0)

        def round_w1(copy, raw, a):
            bf = ring.tile([P, PACK * PASS], BF16, name="w1_bf", tag="bf%d" % a, align_bytes=ALIGN)
            copy(
                out=bf[:].rearrange("p (t m j) -> p m j t", t=PACK, j=PACK),
                in_=raw[:].rearrange("p j (m t) -> p m j t", t=PACK),
            )
            return bf

        def round_w1_on_gpsimd(raw, a):
            bf = ring.tile([P, PACK * PASS], BF16, name="w1_bf", tag="bf%d" % a, align_bytes=ALIGN)
            dst = bf[:].rearrange("p (t m j) -> p t m j", t=PACK, j=PACK)
            src = raw[:].rearrange("p j (m t) -> p t m j", t=PACK)
            ones = one[:].unsqueeze(1).to_broadcast([P, P, PACK])
            for t in range(PACK):
                nc.gpsimd.tensor_tensor(out=dst[:, t], in0=src[:, t], in1=ones, op=ALU.mult)
            return bf

        w1_codes, w1_sc = {}, {}

        def quantise_w1(a, b, bf):
            w1_codes[a, b] = ring.tile([P, PASS], U32, name="w1_codes%d%d" % (a, b), align_bytes=ALIGN)
            w1_sc[a, b] = keep.tile([P, PASS], U8, name="w1_sc%d%d" % (a, b), align_bytes=ALIGN)
            nc.vector.quantize_mx(out=w1_codes[a, b][:].bitcast(FP8X4), scales=w1_sc[a, b][:], in_=bf[:])

        v_words = {}

        def gather_words(a, step):
            v_words[a] = keep.tile([P, S], U32, name="v_words%d" % a, align_bytes=ALIGN)
            for c in range(0, S, step):
                nc.vector.tensor_copy(
                    v_words[a][:, c : c + step],
                    tab_t[a][:].bitcast(U32).indirect(offs_t[:, c // ENTRIES : (c + step) // ENTRIES]),
                )

        halves = [slice(b * PASS, (b + 1) * PASS) for b in range(R_PASSES)]
        raw0 = load_weight(w1, 0, halves[0], "raw0")
        load_table(0)
        raw1 = load_weight(w1, 1, halves[0], "raw1")
        raw2 = load_weight(w1, 2, halves[0], "raw2")
        load_table(1)
        load_table(2)
        load_quiet(0, 0)
        nc.sync.dma_start(pos1_t[:], pos1)
        thr_t = load_rows(thr, "thr_t")
        sharp_t = load_rows(sharp, "sharp_t")
        share_t = load_rows(share, "share_t")
        nc.sync.dma_start(pos2_t[:], pos2)

        bf0 = round_w1(nc.scalar.copy, raw0, 0)
        gather_words(0, S)
        v_sc = keep.tile([P, S], U8, name="v_sc", tag="tab0", align_bytes=ALIGN)
        nc.vector.tensor_copy(v_sc[:], tab_sc[:].indirect(offs_t[:]))
        quantise_w1(0, 0, bf0)
        bf1 = round_w1(nc.scalar.copy, raw1, 1)
        quantise_w1(1, 0, bf1)
        bf2 = round_w1(nc.scalar.copy, raw2, 2)
        gather_words(1, S)
        quantise_w1(2, 0, bf2)
        gather_words(2, BANK)

        slope = ring.tile([P, R_PASSES, PACK], F32, name="slope", align_bytes=ALIGN)
        nc.gpsimd.tensor_tensor(out=slope[:], in0=sharp_t[:], in1=share_t[:], op=ALU.mult)
        top = ring.tile([P, R_PASSES, PACK], F32, name="top", align_bytes=ALIGN)
        c_bias = keep.tile([P, R_PASSES, PACK], F32, name="c_bias")

        def scores(b, t):
            h = ring.tile([P, S], F32, name="h", tag="h%d%d" % (b, t), align_bytes=ALIGN)
            for s in range(S // BANK):
                cols = slice(s * BANK, (s + 1) * BANK)
                acc = psum.tile([P, BANK], F32, name="acc", tag="bank")
                for a in range(K_PASSES):
                    nc.tensor.matmul_mx(
                        out=acc[:],
                        lhsT=w1_codes[a, b][:, t * P : (t + 1) * P].bitcast(FP8X4),
                        lhsT_scale=w1_sc[a, b][:, t * P : (t + 1) * P],
                        rhs=v_words[a][:, cols].bitcast(FP8X4),
                        rhs_scale=v_sc[SCALE_ROWS * a : P, cols],
                        start=(a == 0),
                        stop=(a == K_PASSES - 1),
                    )
                nc.vector.tensor_tensor(out=h[:, cols], in0=acc[:], in1=quiet_t[b, t][:, cols], op=ALU.max)
            nc.vector.tensor_reduce(out=top[:, b, t : t + 1], in_=h[:], axis=AXIS.X, op=ALU.max)
            nc.vector.tensor_scalar(
                out=c_bias[:, b, t : t + 1], in0=top[:, b, t : t + 1], scalar1=slope[:, b, t : t + 1],
                scalar2=-1.0, op0=ALU.mult, op1=ALU.mult,
            )
            return h

        def looks(b, t, h, a_t, c_t, cols):
            entries = slice(cols.start // ENTRIES, cols.stop // ENTRIES)
            nc.scalar.activation(
                out=a_t[:, t, :], in_=h[:].indirect(pos1_t[:, entries]), func=ACT.Sigmoid,
                bias=thr_t[:, b, t : t + 1],
            )
            nc.scalar.activation(
                out=c_t[:, t, :], in_=h[:].indirect(pos2_t[:, entries]), func=ACT.Sigmoid,
                bias=c_bias[:, b, t : t + 1], scale=sharp_t[:, b, t : t + 1],
            )

        w1_raw = [load_weight(w1, 0, halves[1], "raw3")]
        load_quiet(0, 1)
        side_t = load_rows(side, "side_t")
        w1_raw.append(load_weight(w1, 1, halves[1], "raw0"))
        load_quiet(0, 2)
        load_quiet(0, 3)
        w1_raw.append(load_weight(w1, 2, halves[1], "raw1"))
        w4_raw = [load_weight(w4, 0, slice(0, N), "raw2")]
        load_quiet(1, 0)
        w4_raw.append(load_weight(w4, 1, slice(0, N), "raw3"))
        for t in range(1, PACK):
            load_quiet(1, t)
        for quad in range(QUADS):
            rows = w3_scales[:, SCALE_ROWS * quad : SCALE_ROWS * (quad + 1), :]
            nc.sync.dma_start(
                out=w3_sc[32 * quad : 32 * quad + SCALE_ROWS, :, :].bitcast(I32),
                in_=rows.rearrange("b r n -> r b n").bitcast(I32),
            )
        nc.sync.dma_start(out=w3_t[:].bitcast(I32), in_=w3_words.rearrange("b p n -> p b n").bitcast(I32))
        duty_t = ring.tile([P, N_TILES, M], F32, name="duty_t", tag="raw0")
        nc.sync.dma_start(out=duty_t[:], in_=duty.rearrange("(n p) m -> p n m", p=P))

        w1_bf = [round_w1_on_gpsimd(w1_raw[0], 0), round_w1(nc.scalar.copy, w1_raw[1], 1)]
        h0 = [scores(0, t) for t in range(PACK - 1)]
        w1_bf.append(round_w1(nc.vector.tensor_copy, w1_raw[2], 2))
        for a in range(K_PASSES):
            quantise_w1(a, 1, w1_bf[a])
        h0.append(scores(0, PACK - 1))

        a0 = ring.tile([P, PACK, M], F32, name="a0", align_bytes=ALIGN)
        c0 = ring.tile([P, PACK, M], F32, name="c0", align_bytes=ALIGN)
        diff0 = ring.tile([P, PACK, M], F32, name="diff0", tag="bf2", align_bytes=ALIGN)
        for t in range(PACK):
            looks(0, t, h0[t], a0, c0, slice(0, M))
            nc.gpsimd.tensor_tensor(out=diff0[:, t, :], in0=a0[:, t, :], in1=c0[:, t, :], op=ALU.subtract)

        a1, c1 = [], []
        for u in range(2):
            a1.append(ring.tile([P, PACK, HALF], F32, name="a1%d" % u, align_bytes=ALIGN))
            c1.append(ring.tile([P, PACK, HALF], F32, name="c1%d" % u, align_bytes=ALIGN))
        for t in range(PACK):
            h = scores(1, t)
            for u in range(2):
                looks(1, t, h, a1[u], c1[u], slice(u * HALF, (u + 1) * HALF))

        def interleave(copy, src, dst):
            copy(
                out=dst[:].rearrange("p (c i j) -> p c j i", i=LINE, j=PACK),
                in_=src[:].rearrange("p j (c i) -> p c j i", i=LINE),
            )

        w4_bf = [
            ring.tile([P, PACK * N], BF16, name="w4_bf0", tag="slope", align_bytes=ALIGN),
            ring.tile([P, PACK * N], BF16, name="w4_bf1", tag="h13", align_bytes=ALIGN),
        ]
        interleave(nc.vector.tensor_copy, w4_raw[0], w4_bf[0])
        interleave(nc.scalar.copy, w4_raw[1], w4_bf[1])
        w4_codes, w4_sc = {}, {}

        def quantise_w4(b, tag):
            w4_codes[b] = ring.tile([P, N], U32, name="w4_codes", tag=tag, align_bytes=ALIGN)
            w4_sc[b] = keep.tile([P, N], U8, name="w4_sc%d" % b, align_bytes=ALIGN)
            for cols in (slice(0, WIDE_QUANT), slice(WIDE_QUANT, N)):
                nc.vector.quantize_mx(
                    out=w4_codes[b][:, cols].bitcast(FP8X4), scales=w4_sc[b][:, cols],
                    in_=w4_bf[b][:, PACK * cols.start : PACK * cols.stop],
                )

        def quantise_d(bf, width, name, tag):
            codes = ring.tile([P, width], U32, name="d_codes", tag=tag, align_bytes=ALIGN)
            sc = keep.tile([P, width], U8, name=name, align_bytes=ALIGN)
            nc.vector.quantize_mx(out=codes[:].bitcast(FP8X4), scales=sc[:], in_=bf[:])
            return codes, sc

        def difference(u, tag):
            diff = ring.tile([P, PACK, HALF], F32, name="diff1", tag=tag, align_bytes=ALIGN)
            nc.vector.tensor_tensor(out=diff[:], in0=a1[u][:], in1=c1[u][:], op=ALU.subtract)
            return diff

        quantise_w4(0, "quiet11")

        d0_bf = ring.tile([P, M * PACK], BF16, name="d0_bf", tag="h01", align_bytes=ALIGN)
        for c in range(0, M, P):
            nc.gpsimd.tensor_tensor(
                out=d0_bf[:].rearrange("p (m t) -> p m t", t=PACK)[:, c : c + P],
                in0=diff0[:].rearrange("p t m -> p m t")[:, c : c + P],
                in1=side_t[:, 0, :].unsqueeze(1).to_broadcast([P, P, PACK]),
                op=ALU.mult,
            )
        d0 = quantise_d(d0_bf, M, "d0_sc", "top")

        diff = difference(0, "quiet01")
        rounded = ring.tile([P, PACK, HALF], BF16, name="rounded", tag="quiet10", align_bytes=ALIGN)
        for t in range(PACK):
            nc.vector.tensor_scalar(
                out=rounded[:, t, :], in0=diff[:, t, :], scalar1=side_t[:, 1, t : t + 1], scalar2=None,
                op0=ALU.mult,
            )
        d1_bf = ring.tile([P, HALF * PACK], BF16, name="d1_bf", tag="quiet02", align_bytes=ALIGN)
        interleave(nc.vector.tensor_copy, rounded, d1_bf)
        d1 = [quantise_d(d1_bf, HALF, "d10_sc", "d10_codes")]

        diff = difference(1, "quiet00")
        quantise_w4(1, "quiet12")
        rounded = ring.tile([P, PACK, HALF], BF16, name="rounded", tag="h00", align_bytes=ALIGN)
        for t in range(PACK):
            nc.scalar.activation(
                out=rounded[:, t, :], in_=diff[:, t, :], func=ACT.Copy, scale=side_t[:, 1, t : t + 1]
            )
        d1_bf = ring.tile([P, HALF * PACK], BF16, name="d1_bf", tag="quiet03", align_bytes=ALIGN)
        interleave(nc.scalar.copy, rounded, d1_bf)
        d1.append(quantise_d(d1_bf, HALF, "d11_sc", "d11_codes"))

        def reading(acc, n0, n1, codes, sc, rhs, rhs_sc):
            for n in range(n0, n1):
                for b in range(R_PASSES):
                    nc.tensor.matmul_mx(
                        out=acc[:, (n - n0) * HALF : (n - n0 + 1) * HALF],
                        lhsT=codes(b, n), lhsT_scale=sc(b, n), rhs=rhs[b], rhs_scale=rhs_sc[b],
                        start=(b == 0), stop=(b == R_PASSES - 1),
                    )

        for u in range(2):
            cols = slice(u * HALF, (u + 1) * HALF)
            rhs = [d0[0][:, cols].bitcast(FP8X4), d1[u][0][:].bitcast(FP8X4)]
            rhs_sc = [d0[1][:, cols], d1[u][1][:]]
            for n0, n1 in GROUPS:
                pair = n1 - n0 == 2
                bank = psum.tile([P, BANK], F32, name="acc", tag="bank")
                if pair:
                    second_bank = psum.tile([P, BANK], F32, name="acc", tag="bank")
                    acc_alarm, acc_trend = bank[:], second_bank[:]
                else:
                    acc_alarm, acc_trend = bank[:, 0:HALF], bank[:, HALF:BANK]
                reading(
                    acc_alarm, n0, n1,
                    lambda b, n: w3_t[:, b, 2 * n * P : 2 * (n + 1) * P].bitcast(FP4X4),
                    lambda b, n: w3_sc[:, b, n * P : (n + 1) * P], rhs, rhs_sc,
                )
                reading(
                    acc_trend, n0, n1,
                    lambda b, n: w4_codes[b][:, n * P : (n + 1) * P].bitcast(FP8X4),
                    lambda b, n: w4_sc[b][:, n * P : (n + 1) * P], rhs, rhs_sc,
                )
                alarm = ring.tile([P, (n1 - n0) * HALF], F32, name="alarm", bufs=3)
                nc.scalar.activation(out=alarm[:], in_=acc_alarm, func=ACT.Tanh)
                by_tile = alarm[:].rearrange("p (n m) -> p n m", m=HALF)
                engine = nc.vector if pair else nc.gpsimd
                engine.tensor_tensor(out=by_tile, in0=by_tile, in1=duty_t[:, n0:n1, cols], op=ALU.mult)
                result = ring.tile([P, (n1 - n0) * HALF], F32, name="result", bufs=4)
                nc.vector.tensor_tensor(out=result[:], in0=acc_trend, in1=alarm[:], op=ALU.add)
                nc.sync.dma_start(
                    out=out[n0 * P : n1 * P, cols].rearrange("(n p) m -> p n m", p=P),
                    in_=result[:].rearrange("p (n m) -> p n m", m=HALF),
                )
